import numpy as np
import ml_dtypes


def mxq(x, axis, fmt="e4m3"):
    dtype, down = {"e4m3": (ml_dtypes.float8_e4m3fn, 7), "e5m2": (ml_dtypes.float8_e5m2, 14)}[fmt]
    v = np.moveaxis(np.asarray(x, np.float32).astype(ml_dtypes.bfloat16).astype(np.float64), axis, -1)
    blocks = v.reshape(v.shape[:-1] + (-1, 32))
    amax = np.abs(blocks).max(-1, keepdims=True)
    byte = np.maximum(np.where(amax > 0, np.frexp(amax)[1] - 1 + 127, 0) - down, 1)
    scale = np.exp2(byte - 127.0)
    codes = (blocks / scale).astype(np.float32).astype(dtype).astype(np.float64)
    return np.moveaxis((codes * scale).reshape(v.shape), -1, axis)


WIDE = False


def mx_kscale(k):
    if not WIDE:
        return np.ones(k)
    levels = np.array([10, -10, 5, -5, 0])
    if k % 512:
        return np.exp2(np.random.permutation(np.resize(levels, k // 32))).repeat(32)
    a = np.empty((k // 512, 16))
    for p in range(k // 512):
        a[p, :8] = np.random.permutation(np.resize(levels, 8))
        for g in range(8):
            far = levels[np.abs(levels - a[p, g]) >= 10]
            a[p, g + 8] = far[np.random.randint(len(far))]
    return np.exp2(a.ravel()).repeat(32)


def f64(x):
    return np.asarray(x).astype(np.float64)


def striped(idx):
    return np.tile(np.asarray(idx).reshape(-1, 16).T, (8, 1)).astype(np.uint16)


def unstriped(offs):
    return offs[:16].T.reshape(-1).astype(np.int64)


E2M1 = np.array([0.0, 0.5, 1.0, 1.5, 2.0, 3.0, 4.0, 6.0, -0.0, -0.5, -1.0, -1.5, -2.0, -3.0, -4.0, -6.0])


def pack_weight(w, fmt):
    k, n = w.shape
    w = f64(np.asarray(w, np.float32).astype(ml_dtypes.bfloat16)).reshape(k // 32, 32, n)
    amax = np.abs(w).max(1)
    if fmt == "e4m3":
        byte = np.frexp(amax)[1] - 1 + 127 - 7
    else:
        mant, ex = np.frexp(amax / 6.0)
        byte = np.where(mant > 0.5, ex, ex - 1) + 127
    byte = np.clip(np.where(amax > 0, byte, 1), 1, 254)
    scaled = (w * np.exp2(127.0 - byte)[:, None, :]).reshape(k, n).astype(np.float32)
    by_word = np.ascontiguousarray(scaled.reshape(k // 512, 128, 4, n).transpose(0, 1, 3, 2))
    if fmt == "e4m3":
        words = by_word.astype(ml_dtypes.float8_e4m3fn).view(np.uint8)
    else:
        c = by_word.astype(ml_dtypes.float4_e2m1fn).view(np.uint8) & 0xF
        words = (c[..., 0::2] | (c[..., 1::2] << 4)).reshape(k // 512, 128, 2 * n)
    return np.ascontiguousarray(words), np.ascontiguousarray(byte.astype(np.uint8).reshape(k // 512, 16, n))


def unpack_weight(words, scales, fmt):
    g, _, n = scales.shape
    words = np.ascontiguousarray(words).reshape(g, 128, n, -1)
    if fmt == "e4m3":
        vals = words.view(ml_dtypes.float8_e4m3fn).astype(np.float64)
    else:
        nib = np.empty((g, 128, n, 4), np.uint8)
        nib[..., 0::2] = words & 0xF
        nib[..., 1::2] = words >> 4
        vals = E2M1[nib]
    vals = vals * np.repeat(np.exp2(scales.astype(np.float64) - 127.0), 8, axis=1)[..., None]
    return vals.transpose(0, 1, 3, 2).reshape(g * 512, n)


B, N, T, D, NQ = 1, 512, 2048, 1024, 128


def setup_inputs():
    n = np.random.standard_normal
    idx = np.random.permutation(T)[:B * N]
    s = mx_kscale(D)[:, None]
    kp = pack_weight(n((D, T)) / s, "e2m1")
    return {
        "qT": (n((B, D, NQ)) * s * (1.00 / np.sqrt(D))).astype(np.float32),
        "k_words": np.ascontiguousarray(kp[0].reshape(1, 2, 128, T, 2).transpose(0, 2, 3, 1, 4)).reshape(1, 128, T, 4),
        "k_scales": kp[1],
        "mk": (np.random.uniform(size=(B, NQ, N)) < 0.8).astype(np.float32),
        "offs": striped(idx),
    }


def reference(qT, k_words, k_scales, mk, offs):
    idx = unstriped(offs)
    pick = lambda x, which: x[:, which].reshape(x.shape[0], B, -1).transpose(1, 0, 2)
    k = unpack_weight(k_words.reshape(1, 128, T, 2, 2).transpose(0, 3, 1, 2, 4).reshape(2, 128, 2 * T), k_scales, "e2m1")
    kg = pick(k, idx)
    qq = mxq(f64(qT), 1, "e4m3")
    a = qq.transpose(0, 2, 1) @ kg
    m = np.max(a, axis=-1, keepdims=True)
    e = np.exp(a - m) * f64(mk)
    y = e / np.sum(e, axis=-1, keepdims=True)
    return y

@@ -1,0 +1,112 @@
+from contextlib import ExitStack
+
+import concourse.mybir as mybir
+
+F32 = mybir.dt.float32
+BF16 = mybir.dt.bfloat16
+I32 = mybir.dt.int32
+U32 = mybir.dt.uint32
+U16 = mybir.dt.uint16
+U8 = mybir.dt.uint8
+FP8X4 = mybir.dt.float8_e4m3fn_x4
+FP4X4 = mybir.dt.float4_e2m1fn_x4
+ALU = mybir.AluOpType
+ACT = mybir.ActivationFunctionType
+AX = mybir.AxisListType
+
+P = 128
+PACK = 4
+PASSES = 2
+K_PASS = P * PACK
+NQ = 128
+N = 512
+T = 2048
+
+HIDDEN = 2.0 ** 100
+
+FLOPS = 2 * NQ * N * PASSES * K_PASS
+
+
+def tile_attend_nrm_mask_topk_kernel(tc, qT, k_words, k_scales, mk, offs, out):
+    nc = tc.nc
+    with ExitStack() as ctx:
+        sb = ctx.enter_context(tc.tile_pool(name="sb", bufs=1))
+        psum = ctx.enter_context(tc.psum_pool(name="psum", bufs=1))
+
+        offsets = sb.tile([P, N // 16], U16, name="offsets")
+        nc.sync.dma_start(offsets[:], offs)
+
+        word_pool = sb.tile([P, T], I32, name="word_pool", align_bytes=64)
+        nc.sync.dma_start(word_pool[:], k_words[0].rearrange("p t b -> p (t b)").bitcast(I32))
+
+        scale_pool = sb.tile([P, T], U8, name="scale_pool", align_bytes=64)
+        nc.vector.memset(scale_pool[:].bitcast(I32), 0)
+        scale_rows = k_scales.bitcast(I32).rearrange("o (quad r) t -> r quad o t", r=4)
+        for r in range(4):
+            nc.scalar.dma_start(scale_pool[r:P:16, :].bitcast(I32), scale_rows[r])
+
+        q_raw = sb.tile([P, PASSES, PACK, NQ], F32, name="q_raw", align_bytes=64)
+        for o in range(PASSES):
+            nc.sync.dma_start(q_raw[:, o, :, :], qT[0, o * K_PASS:(o + 1) * K_PASS, :].rearrange("(p j) w -> p j w", j=PACK))
+
+        moved = sb.tile([P, N], U8, name="moved", align_bytes=64)
+        nc.vector.memset(moved[:].bitcast(I32), 0)
+        warm_in = sb.tile([P, 1], F32, name="warm_in")
+        warm_out = sb.tile([P, 1], F32, name="warm_out")
+        nc.vector.memset(warm_in[:], 0.0)
+        nc.scalar.activation(warm_out[:], warm_in[:], ACT.Exp)
+
+        picked = sb.tile([P, N], U8, name="picked", align_bytes=64)
+        nc.vector.tensor_copy(picked[:], scale_pool[:].indirect(offsets[:]))
+        nc.sync.dma_start(moved[0:P - 16, :].bitcast(I32), picked[16:P, :].bitcast(I32))
+        k_planes = [picked, moved]
+
+        mask = sb.tile([P, N], F32, name="mask", align_bytes=64)
+        nc.sync.dma_start(mask[:], mk[0])
+
+        pairs = sb.tile([P, N], U32, name="pairs", align_bytes=64)
+        nc.vector.tensor_copy(pairs[:], word_pool[:].bitcast(U32).indirect(offsets[:]))
+        halves = pairs[:].bitcast(U16).rearrange("p (n h) -> p h n", h=PASSES)
+        k_codes = sb.tile([P, PASSES, 2 * N], U8, name="k_codes", align_bytes=64)
+
+        q_bf = sb.tile([P, PASSES, NQ, PACK], BF16, name="q_bf", align_bytes=64)
+        q_codes = sb.tile([P, PASSES, NQ], U32, name="q_codes", align_bytes=64)
+        q_planes = sb.tile([P, PASSES, NQ], U8, name="q_planes", align_bytes=64)
+        for o in range(PASSES):
+            nc.scalar.copy(q_bf[:, o, :, :], q_raw[:, o, :, :].rearrange("p j w -> p w j"))
+        penalty = sb.tile([P, N], F32, name="penalty", align_bytes=64)
+        nc.scalar.activation(penalty[:], mask[:], ACT.Copy, bias=-HIDDEN, scale=HIDDEN)
+
+        scores = psum.tile([P, N], F32, name="scores")
+        for o in range(PASSES):
+            nc.vector.tensor_copy(k_codes[:, o, :].bitcast(U16), halves[:, o, :])
+            nc.vector.quantize_mx(
+                out=q_codes[:, o, :].bitcast(FP8X4),
+                scales=q_planes[:, o, :],
+                in_=q_bf[:, o, :, :].rearrange("p w j -> p (w j)"),
+            )
+            nc.tensor.matmul_mx(
+                out=scores[:],
+                lhsT=q_codes[:, o, :].bitcast(FP8X4),
+                lhsT_scale=q_planes[:, o, :],
+                rhs=k_codes[:, o, :].bitcast(FP4X4),
+                rhs_scale=k_planes[o][:],
+                start=(o == 0),
+                stop=(o == PASSES - 1),
+            )
+
+        neg_max = sb.tile([P, 1], F32, name="neg_max")
+        nc.vector.tensor_reduce(neg_max[:], scores[:], AX.X, ALU.max, negate=True)
+        masked = sb.tile([P, N], F32, name="masked", align_bytes=64)
+        nc.vector.tensor_tensor(masked[:], scores[:], penalty[:], ALU.add)
+        e = sb.tile([P, N], F32, name="e", align_bytes=64)
+        total = sb.tile([P, 1], F32, name="total")
+        nc.scalar.activation(e[:], masked[:], ACT.Exp, bias=neg_max[:], accum_out=total[:])
+        inv = sb.tile([P, 1], F32, name="inv")
+        nc.vector.reciprocal(inv[:], total[:])
+        res = sb.tile([P, N], F32, name="res", align_bytes=64)
+        half = N // 2
+        nc.vector.tensor_scalar(res[:, :half], e[:, :half], inv[:], None, ALU.mult)
+        nc.sync.dma_start(out[0, :, :half], res[:, :half])
+        nc.scalar.activation(res[:, half:], e[:, half:], ACT.Copy, scale=inv[:])
+        nc.scalar.dma_start(out[0, :, half:], res[:, half:])

@@ -39,7 +39,7 @@ def tile_attend_nrm_mask_topk_kernel(tc, qT, k_words, k_scales, mk, offs, out):
         word_pool = sb.tile([P, T], I32, name="word_pool", align_bytes=64)
         nc.sync.dma_start(word_pool[:], k_words[0].rearrange("p t b -> p (t b)").bitcast(I32))
 
-        scale_pool = sb.tile([P, T], U8, name="scale_pool", align_bytes=64)
+        scale_pool = sb.tile([P, T], U8, name="scale_pool", tag="reused", align_bytes=64)
         nc.vector.memset(scale_pool[:].bitcast(I32), 0)
         scale_rows = k_scales.bitcast(I32).rearrange("o (quad r) t -> r quad o t", r=4)
         for r in range(4):
@@ -52,19 +52,17 @@ def tile_attend_nrm_mask_topk_kernel(tc, qT, k_words, k_scales, mk, offs, out):
         moved = sb.tile([P, N], U8, name="moved", align_bytes=64)
         nc.vector.memset(moved[:].bitcast(I32), 0)
         warm_in = sb.tile([P, 1], F32, name="warm_in")
-        warm_out = sb.tile([P, 1], F32, name="warm_out")
+        mask = sb.tile([P, N], F32, name="mask", align_bytes=64)
         nc.vector.memset(warm_in[:], 0.0)
-        nc.scalar.activation(warm_out[:], warm_in[:], ACT.Exp)
+        nc.scalar.activation(mask[:, 0:1], warm_in[:], ACT.Exp)
+        nc.sync.dma_start(mask[:], mk[0])
 
         picked = sb.tile([P, N], U8, name="picked", align_bytes=64)
         nc.vector.tensor_copy(picked[:], scale_pool[:].indirect(offsets[:]))
         nc.sync.dma_start(moved[0:P - 16, :].bitcast(I32), picked[16:P, :].bitcast(I32))
         k_planes = [picked, moved]
 
-        mask = sb.tile([P, N], F32, name="mask", align_bytes=64)
-        nc.sync.dma_start(mask[:], mk[0])
-
-        pairs = sb.tile([P, N], U32, name="pairs", align_bytes=64)
+        pairs = sb.tile([P, N], U32, name="pairs", tag="reused", align_bytes=64)
         nc.vector.tensor_copy(pairs[:], word_pool[:].bitcast(U32).indirect(offsets[:]))
         halves = pairs[:].bitcast(U16).rearrange("p (n h) -> p h n", h=PASSES)
         k_codes = sb.tile([P, PASSES, 2 * N], U8, name="k_codes", align_bytes=64)
@@ -78,13 +76,18 @@ def tile_attend_nrm_mask_topk_kernel(tc, qT, k_words, k_scales, mk, offs, out):
         nc.scalar.activation(penalty[:], mask[:], ACT.Copy, bias=-HIDDEN, scale=HIDDEN)
 
         scores = psum.tile([P, N], F32, name="scores")
-        for o in range(PASSES):
-            nc.vector.tensor_copy(k_codes[:, o, :].bitcast(U16), halves[:, o, :])
+
+        def quantise(o):
             nc.vector.quantize_mx(
                 out=q_codes[:, o, :].bitcast(FP8X4),
                 scales=q_planes[:, o, :],
                 in_=q_bf[:, o, :, :].rearrange("p w j -> p (w j)"),
             )
+
+        def split(o):
+            nc.vector.tensor_copy(k_codes[:, o, :].bitcast(U16), halves[:, o, :])
+
+        def multiply(o):
             nc.tensor.matmul_mx(
                 out=scores[:],
                 lhsT=q_codes[:, o, :].bitcast(FP8X4),
@@ -94,6 +97,13 @@ def tile_attend_nrm_mask_topk_kernel(tc, qT, k_words, k_scales, mk, offs, out):
                 start=(o == 0),
                 stop=(o == PASSES - 1),
             )
+
+        quantise(0)
+        split(0)
+        multiply(0)
+        split(1)
+        quantise(1)
+        multiply(1)
 
         neg_max = sb.tile([P, 1], F32, name="neg_max")
         nc.vector.tensor_reduce(neg_max[:], scores[:], AX.X, ALU.max, negate=True)

@@ -22,7 +22,7 @@ NQ = 128
 N = 512
 T = 2048
 
-HIDDEN = 2.0 ** 100
+SPAN = 128.0
 
 FLOPS = 2 * NQ * N * PASSES * K_PASS
 
@@ -36,33 +36,42 @@ def tile_attend_nrm_mask_topk_kernel(tc, qT, k_words, k_scales, mk, offs, out):
         offsets = sb.tile([P, N // 16], U16, name="offsets")
         nc.sync.dma_start(offsets[:], offs)
 
+        scale_pool = sb.tile([P, T], U8, name="scale_pool", tag="reused", align_bytes=64)
+        nc.scalar.dma_start(scale_pool[0:32, :].bitcast(I32), k_scales.bitcast(I32).rearrange("o f t -> (o f) t"))
+        nc.vector.memset(scale_pool[32:64, :].bitcast(I32), 0)
+        nc.vector.memset(scale_pool[64:P, :].bitcast(I32), 0)
+
         word_pool = sb.tile([P, T], I32, name="word_pool", align_bytes=64)
         nc.sync.dma_start(word_pool[:], k_words[0].rearrange("p t b -> p (t b)").bitcast(I32))
-
-        scale_pool = sb.tile([P, T], U8, name="scale_pool", tag="reused", align_bytes=64)
-        nc.vector.memset(scale_pool[:].bitcast(I32), 0)
-        scale_rows = k_scales.bitcast(I32).rearrange("o (quad r) t -> r quad o t", r=4)
-        for r in range(4):
-            nc.scalar.dma_start(scale_pool[r:P:16, :].bitcast(I32), scale_rows[r])
 
         q_raw = sb.tile([P, PASSES, PACK, NQ], F32, name="q_raw", align_bytes=64)
         for o in range(PASSES):
             nc.sync.dma_start(q_raw[:, o, :, :], qT[0, o * K_PASS:(o + 1) * K_PASS, :].rearrange("(p j) w -> p j w", j=PACK))
 
-        moved = sb.tile([P, N], U8, name="moved", align_bytes=64)
-        nc.vector.memset(moved[:].bitcast(I32), 0)
+        k_planes = sb.tile([P, PASSES, N], U8, name="k_planes", align_bytes=64)
+        nc.vector.memset(k_planes[:].rearrange("p o n -> p (o n)").bitcast(I32), 0)
         warm_in = sb.tile([P, 1], F32, name="warm_in")
-        mask = sb.tile([P, N], F32, name="mask", align_bytes=64)
+        warm_out = sb.tile([P, 1], F32, name="warm_out")
         nc.vector.memset(warm_in[:], 0.0)
-        nc.scalar.activation(mask[:, 0:1], warm_in[:], ACT.Exp)
-        nc.sync.dma_start(mask[:], mk[0])
+        nc.scalar.activation(warm_out[:], warm_in[:], ACT.Exp)
 
         picked = sb.tile([P, N], U8, name="picked", align_bytes=64)
         nc.vector.tensor_copy(picked[:], scale_pool[:].indirect(offsets[:]))
-        nc.sync.dma_start(moved[0:P - 16, :].bitcast(I32), picked[16:P, :].bitcast(I32))
-        k_planes = [picked, moved]
+        for o in range(PASSES):
+            for quad in range(4):
+                first = 16 * o + 4 * quad
+                rows_out = k_planes[32 * quad:32 * quad + 4, o, :].bitcast(I32)
+                rows_in = picked[first:first + 4, :].bitcast(I32)
+                if first == 32 * quad:
+                    nc.vector.tensor_copy(rows_out, rows_in)
+                else:
+                    queue = nc.sync if quad % 2 == 1 else nc.scalar
+                    queue.dma_start(rows_out, rows_in)
 
-        pairs = sb.tile([P, N], U32, name="pairs", tag="reused", align_bytes=64)
+        mask = sb.tile([P, N], F32, name="mask", tag="reused", align_bytes=64)
+        nc.sync.dma_start(mask[:], mk[0])
+
+        pairs = sb.tile([P, N], U32, name="pairs", align_bytes=64)
         nc.vector.tensor_copy(pairs[:], word_pool[:].bitcast(U32).indirect(offsets[:]))
         halves = pairs[:].bitcast(U16).rearrange("p (n h) -> p h n", h=PASSES)
         k_codes = sb.tile([P, PASSES, 2 * N], U8, name="k_codes", align_bytes=64)
@@ -72,8 +81,6 @@ def tile_attend_nrm_mask_topk_kernel(tc, qT, k_words, k_scales, mk, offs, out):
         q_planes = sb.tile([P, PASSES, NQ], U8, name="q_planes", align_bytes=64)
         for o in range(PASSES):
             nc.scalar.copy(q_bf[:, o, :, :], q_raw[:, o, :, :].rearrange("p j w -> p w j"))
-        penalty = sb.tile([P, N], F32, name="penalty", align_bytes=64)
-        nc.scalar.activation(penalty[:], mask[:], ACT.Copy, bias=-HIDDEN, scale=HIDDEN)
 
         scores = psum.tile([P, N], F32, name="scores")
 
@@ -93,25 +100,26 @@ def tile_attend_nrm_mask_topk_kernel(tc, qT, k_words, k_scales, mk, offs, out):
                 lhsT=q_codes[:, o, :].bitcast(FP8X4),
                 lhsT_scale=q_planes[:, o, :],
                 rhs=k_codes[:, o, :].bitcast(FP4X4),
-                rhs_scale=k_planes[o][:],
+                rhs_scale=k_planes[:, o, :],
                 start=(o == 0),
                 stop=(o == PASSES - 1),
             )
 
-        quantise(0)
         split(0)
+        quantise(0)
         multiply(0)
         split(1)
         quantise(1)
         multiply(1)
 
-        neg_max = sb.tile([P, 1], F32, name="neg_max")
-        nc.vector.tensor_reduce(neg_max[:], scores[:], AX.X, ALU.max, negate=True)
-        masked = sb.tile([P, N], F32, name="masked", align_bytes=64)
-        nc.vector.tensor_tensor(masked[:], scores[:], penalty[:], ALU.add)
+        lowered = sb.tile([P, N], F32, name="lowered", align_bytes=64)
+        floor = sb.tile([P, 1], F32, name="floor")
+        nc.vector.tensor_scalar(lowered[:], scores[:], SPAN, None, ALU.subtract, ALU.max, accum_out=floor[:])
+        lifted = sb.tile([P, N], F32, name="lifted", align_bytes=64)
+        nc.vector.scalar_tensor_tensor(lifted[:], scores[:], floor[:], mask[:], ALU.subtract, ALU.mult)
         e = sb.tile([P, N], F32, name="e", align_bytes=64)
         total = sb.tile([P, 1], F32, name="total")
-        nc.scalar.activation(e[:], masked[:], ACT.Exp, bias=neg_max[:], accum_out=total[:])
+        nc.scalar.activation(e[:], lifted[:], ACT.Exp, bias=-SPAN, accum_out=total[:])
         inv = sb.tile([P, 1], F32, name="inv")
         nc.vector.reciprocal(inv[:], total[:])
         res = sb.tile([P, N], F32, name="res", align_bytes=64)

@@ -72,7 +72,12 @@ def tile_attend_nrm_mask_topk_kernel(tc, qT, k_words, k_scales, mk, offs, out):
         nc.sync.dma_start(mask[:], mk[0])
 
         pairs = sb.tile([P, N], U32, name="pairs", align_bytes=64)
-        nc.vector.tensor_copy(pairs[:], word_pool[:].bitcast(U32).indirect(offsets[:]))
+        half = N // 2
+        for h in range(2):
+            nc.vector.tensor_copy(
+                pairs[:, h * half:(h + 1) * half],
+                word_pool[:].bitcast(U32).indirect(offsets[:, h * half // 16:(h + 1) * half // 16]),
+            )
         halves = pairs[:].bitcast(U16).rearrange("p (n h) -> p h n", h=PASSES)
         k_codes = sb.tile([P, PASSES, 2 * N], U8, name="k_codes", align_bytes=64)
 
@@ -91,8 +96,8 @@ def tile_attend_nrm_mask_topk_kernel(tc, qT, k_words, k_scales, mk, offs, out):
                 in_=q_bf[:, o, :, :].rearrange("p w j -> p (w j)"),
             )
 
-        def split(o):
-            nc.vector.tensor_copy(k_codes[:, o, :].bitcast(U16), halves[:, o, :])
+        def split(o, slots):
+            nc.vector.tensor_copy(k_codes[:, o, :].bitcast(U16)[:, slots], halves[:, o, slots])
 
         def multiply(o):
             nc.tensor.matmul_mx(
@@ -105,25 +110,26 @@ def tile_attend_nrm_mask_topk_kernel(tc, qT, k_words, k_scales, mk, offs, out):
                 stop=(o == PASSES - 1),
             )
 
-        split(0)
+        split(0, slice(0, half))
         quantise(0)
+        split(0, slice(half, N))
         multiply(0)
-        split(1)
+        split(1, slice(0, N))
         quantise(1)
         multiply(1)
 
-        lowered = sb.tile([P, N], F32, name="lowered", align_bytes=64)
-        floor = sb.tile([P, 1], F32, name="floor")
-        nc.vector.tensor_scalar(lowered[:], scores[:], SPAN, None, ALU.subtract, ALU.max, accum_out=floor[:])
+        neg_max = sb.tile([P, 1], F32, name="neg_max")
+        nc.vector.tensor_reduce(neg_max[:], scores[:], AX.X, ALU.max, negate=True)
         lifted = sb.tile([P, N], F32, name="lifted", align_bytes=64)
-        nc.vector.scalar_tensor_tensor(lifted[:], scores[:], floor[:], mask[:], ALU.subtract, ALU.mult)
+        nc.vector.scalar_tensor_tensor(lifted[:], mask[:], SPAN, scores[:], ALU.mult, ALU.add)
+        shift = sb.tile([P, 1], F32, name="shift")
+        nc.scalar.activation(shift[:], neg_max[:], ACT.Copy, bias=-SPAN)
         e = sb.tile([P, N], F32, name="e", align_bytes=64)
         total = sb.tile([P, 1], F32, name="total")
-        nc.scalar.activation(e[:], lifted[:], ACT.Exp, bias=-SPAN, accum_out=total[:])
+        nc.scalar.activation(e[:], lifted[:], ACT.Exp, bias=shift[:], accum_out=total[:])
         inv = sb.tile([P, 1], F32, name="inv")
         nc.vector.reciprocal(inv[:], total[:])
         res = sb.tile([P, N], F32, name="res", align_bytes=64)
-        half = N // 2
         nc.vector.tensor_scalar(res[:, :half], e[:, :half], inv[:], None, ALU.mult)
         nc.sync.dma_start(out[0, :, :half], res[:, :half])
         nc.scalar.activation(res[:, half:], e[:, half:], ACT.Copy, scale=inv[:])

@@ -36,7 +36,7 @@ def tile_attend_nrm_mask_topk_kernel(tc, qT, k_words, k_scales, mk, offs, out):
         offsets = sb.tile([P, N // 16], U16, name="offsets")
         nc.sync.dma_start(offsets[:], offs)
 
-        scale_pool = sb.tile([P, T], U8, name="scale_pool", tag="reused", align_bytes=64)
+        scale_pool = sb.tile([P, T], U8, name="scale_pool", align_bytes=64)
         nc.scalar.dma_start(scale_pool[0:32, :].bitcast(I32), k_scales.bitcast(I32).rearrange("o f t -> (o f) t"))
         nc.vector.memset(scale_pool[32:64, :].bitcast(I32), 0)
         nc.vector.memset(scale_pool[64:P, :].bitcast(I32), 0)
@@ -44,12 +44,15 @@ def tile_attend_nrm_mask_topk_kernel(tc, qT, k_words, k_scales, mk, offs, out):
         word_pool = sb.tile([P, T], I32, name="word_pool", align_bytes=64)
         nc.sync.dma_start(word_pool[:], k_words[0].rearrange("p t b -> p (t b)").bitcast(I32))
 
-        q_raw = sb.tile([P, PASSES, PACK, NQ], F32, name="q_raw", align_bytes=64)
+        q_raw = [
+            sb.tile([P, PACK, NQ], F32, name=f"q_raw{o}", tag=f"q_raw{o}", align_bytes=64) for o in range(PASSES)
+        ]
         for o in range(PASSES):
-            nc.sync.dma_start(q_raw[:, o, :, :], qT[0, o * K_PASS:(o + 1) * K_PASS, :].rearrange("(p j) w -> p j w", j=PACK))
+            nc.sync.dma_start(q_raw[o][:], qT[0, o * K_PASS:(o + 1) * K_PASS, :].rearrange("(p j) w -> p j w", j=PACK))
 
-        k_planes = sb.tile([P, PASSES, N], U8, name="k_planes", align_bytes=64)
-        nc.vector.memset(k_planes[:].rearrange("p o n -> p (o n)").bitcast(I32), 0)
+        k_planes = [sb.tile([P, N], U8, name=f"k_plane{o}", align_bytes=64) for o in range(PASSES)]
+        for o in range(PASSES):
+            nc.vector.memset(k_planes[o][:].bitcast(I32), 0)
         warm_in = sb.tile([P, 1], F32, name="warm_in")
         warm_out = sb.tile([P, 1], F32, name="warm_out")
         nc.vector.memset(warm_in[:], 0.0)
@@ -60,16 +63,13 @@ def tile_attend_nrm_mask_topk_kernel(tc, qT, k_words, k_scales, mk, offs, out):
         for o in range(PASSES):
             for quad in range(4):
                 first = 16 * o + 4 * quad
-                rows_out = k_planes[32 * quad:32 * quad + 4, o, :].bitcast(I32)
+                rows_out = k_planes[o][32 * quad:32 * quad + 4, :].bitcast(I32)
                 rows_in = picked[first:first + 4, :].bitcast(I32)
                 if first == 32 * quad:
                     nc.vector.tensor_copy(rows_out, rows_in)
                 else:
-                    queue = nc.sync if quad % 2 == 1 else nc.scalar
+                    queue = nc.sync if o == 1 else nc.scalar
                     queue.dma_start(rows_out, rows_in)
-
-        mask = sb.tile([P, N], F32, name="mask", tag="reused", align_bytes=64)
-        nc.sync.dma_start(mask[:], mk[0])
 
         pairs = sb.tile([P, N], U32, name="pairs", align_bytes=64)
         half = N // 2
@@ -79,13 +79,17 @@ def tile_attend_nrm_mask_topk_kernel(tc, qT, k_words, k_scales, mk, offs, out):
                 word_pool[:].bitcast(U32).indirect(offsets[:, h * half // 16:(h + 1) * half // 16]),
             )
         halves = pairs[:].bitcast(U16).rearrange("p (n h) -> p h n", h=PASSES)
-        k_codes = sb.tile([P, PASSES, 2 * N], U8, name="k_codes", align_bytes=64)
 
-        q_bf = sb.tile([P, PASSES, NQ, PACK], BF16, name="q_bf", align_bytes=64)
+        q_bf = [
+            sb.tile([P, NQ, PACK], BF16, name=f"q_bf{o}", tag=f"q_bf{o}", align_bytes=64) for o in range(PASSES)
+        ]
         q_codes = sb.tile([P, PASSES, NQ], U32, name="q_codes", align_bytes=64)
         q_planes = sb.tile([P, PASSES, NQ], U8, name="q_planes", align_bytes=64)
         for o in range(PASSES):
-            nc.scalar.copy(q_bf[:, o, :, :], q_raw[:, o, :, :].rearrange("p j w -> p w j"))
+            nc.scalar.copy(q_bf[o][:], q_raw[o][:].rearrange("p j w -> p w j"))
+
+        mask = sb.tile([P, N], F32, name="mask", tag="q_raw0", align_bytes=64)
+        nc.sync.dma_start(mask[:], mk[0])
 
         scores = psum.tile([P, N], F32, name="scores")
 
@@ -93,27 +97,29 @@ def tile_attend_nrm_mask_topk_kernel(tc, qT, k_words, k_scales, mk, offs, out):
             nc.vector.quantize_mx(
                 out=q_codes[:, o, :].bitcast(FP8X4),
                 scales=q_planes[:, o, :],
-                in_=q_bf[:, o, :, :].rearrange("p w j -> p (w j)"),
+                in_=q_bf[o][:].rearrange("p w j -> p (w j)"),
             )
 
         def split(o, slots):
-            nc.vector.tensor_copy(k_codes[:, o, :].bitcast(U16)[:, slots], halves[:, o, slots])
+            nc.vector.tensor_copy(k_codes[o][:].bitcast(U16)[:, slots], halves[:, o, slots])
 
         def multiply(o):
             nc.tensor.matmul_mx(
                 out=scores[:],
                 lhsT=q_codes[:, o, :].bitcast(FP8X4),
                 lhsT_scale=q_planes[:, o, :],
-                rhs=k_codes[:, o, :].bitcast(FP4X4),
-                rhs_scale=k_planes[:, o, :],
+                rhs=k_codes[o][:].bitcast(FP4X4),
+                rhs_scale=k_planes[o][:],
                 start=(o == 0),
                 stop=(o == PASSES - 1),
             )
 
+        k_codes = [sb.tile([P, 2 * N], U8, name="k_codes0", align_bytes=64)]
         split(0, slice(0, half))
-        quantise(0)
         split(0, slice(half, N))
+        quantise(0)
         multiply(0)
+        k_codes.append(sb.tile([P, 2 * N], U8, name="k_codes1", tag="q_bf0", align_bytes=64))
         split(1, slice(0, N))
         quantise(1)
         multiply(1)

@@ -37,7 +37,7 @@ def tile_attend_nrm_mask_topk_kernel(tc, qT, k_words, k_scales, mk, offs, out):
         nc.sync.dma_start(offsets[:], offs)
 
         scale_pool = sb.tile([P, T], U8, name="scale_pool", align_bytes=64)
-        nc.scalar.dma_start(scale_pool[0:32, :].bitcast(I32), k_scales.bitcast(I32).rearrange("o f t -> (o f) t"))
+        nc.scalar.dma_start(scale_pool[0:32, :].bitcast(I32), k_scales.bitcast(I32).rearrange("o f t -> f o t"))
         nc.vector.memset(scale_pool[32:64, :].bitcast(I32), 0)
         nc.vector.memset(scale_pool[64:P, :].bitcast(I32), 0)
 
@@ -50,9 +50,8 @@ def tile_attend_nrm_mask_topk_kernel(tc, qT, k_words, k_scales, mk, offs, out):
         for o in range(PASSES):
             nc.sync.dma_start(q_raw[o][:], qT[0, o * K_PASS:(o + 1) * K_PASS, :].rearrange("(p j) w -> p j w", j=PACK))
 
-        k_planes = [sb.tile([P, N], U8, name=f"k_plane{o}", align_bytes=64) for o in range(PASSES)]
-        for o in range(PASSES):
-            nc.vector.memset(k_planes[o][:].bitcast(I32), 0)
+        k_planes = sb.tile([P, PASSES * N], U8, name="k_planes", align_bytes=64)
+        nc.vector.memset(k_planes[:].bitcast(I32), 0)
         warm_in = sb.tile([P, 1], F32, name="warm_in")
         warm_out = sb.tile([P, 1], F32, name="warm_out")
         nc.vector.memset(warm_in[:], 0.0)
@@ -60,16 +59,8 @@ def tile_attend_nrm_mask_topk_kernel(tc, qT, k_words, k_scales, mk, offs, out):
 
         picked = sb.tile([P, N], U8, name="picked", align_bytes=64)
         nc.vector.tensor_copy(picked[:], scale_pool[:].indirect(offsets[:]))
-        for o in range(PASSES):
-            for quad in range(4):
-                first = 16 * o + 4 * quad
-                rows_out = k_planes[o][32 * quad:32 * quad + 4, :].bitcast(I32)
-                rows_in = picked[first:first + 4, :].bitcast(I32)
-                if first == 32 * quad:
-                    nc.vector.tensor_copy(rows_out, rows_in)
-                else:
-                    queue = nc.sync if o == 1 else nc.scalar
-                    queue.dma_start(rows_out, rows_in)
+        for quad in range(4):
+            nc.scalar.dma_start(k_planes[32 * quad:32 * quad + 4, :].bitcast(I32), picked[8 * quad:8 * quad + 8, :].bitcast(I32))
 
         pairs = sb.tile([P, N], U32, name="pairs", align_bytes=64)
         half = N // 2
@@ -86,7 +77,9 @@ def tile_attend_nrm_mask_topk_kernel(tc, qT, k_words, k_scales, mk, offs, out):
         q_codes = sb.tile([P, PASSES, NQ], U32, name="q_codes", align_bytes=64)
         q_planes = sb.tile([P, PASSES, NQ], U8, name="q_planes", align_bytes=64)
         for o in range(PASSES):
-            nc.scalar.copy(q_bf[o][:], q_raw[o][:].rearrange("p j w -> p w j"))
+            nc.scalar.copy(
+                q_bf[o][:].rearrange("p (c i) j -> p c j i", i=4), q_raw[o][:].rearrange("p j (c i) -> p c j i", i=4)
+            )
 
         mask = sb.tile([P, N], F32, name="mask", tag="q_raw0", align_bytes=64)
         nc.sync.dma_start(mask[:], mk[0])
@@ -109,7 +102,7 @@ def tile_attend_nrm_mask_topk_kernel(tc, qT, k_words, k_scales, mk, offs, out):
                 lhsT=q_codes[:, o, :].bitcast(FP8X4),
                 lhsT_scale=q_planes[:, o, :],
                 rhs=k_codes[o][:].bitcast(FP4X4),
-                rhs_scale=k_planes[o][:],
+                rhs_scale=k_planes[:, o * N:(o + 1) * N],
                 start=(o == 0),
                 stop=(o == PASSES - 1),
             )

@@ -42,13 +42,17 @@ def tile_attend_nrm_mask_topk_kernel(tc, qT, k_words, k_scales, mk, offs, out):
         nc.vector.memset(scale_pool[64:P, :].bitcast(I32), 0)
 
         word_pool = sb.tile([P, T], I32, name="word_pool", align_bytes=64)
-        nc.sync.dma_start(word_pool[:], k_words[0].rearrange("p t b -> p (t b)").bitcast(I32))
+        words = k_words[0].rearrange("p t b -> p (t b)").bitcast(I32)
+        for tokens in (slice(0, T // 4), slice(T // 4, T // 2), slice(T // 2, T)):
+            nc.sync.dma_start(word_pool[:, tokens], words[:, tokens])
 
         q_raw = [
             sb.tile([P, PACK, NQ], F32, name=f"q_raw{o}", tag=f"q_raw{o}", align_bytes=64) for o in range(PASSES)
         ]
         for o in range(PASSES):
             nc.sync.dma_start(q_raw[o][:], qT[0, o * K_PASS:(o + 1) * K_PASS, :].rearrange("(p j) w -> p j w", j=PACK))
+        mask = sb.tile([P, N], F32, name="mask", align_bytes=64)
+        nc.sync.dma_start(mask[:], mk[0])
 
         k_planes = sb.tile([P, PASSES * N], U8, name="k_planes", align_bytes=64)
         nc.vector.memset(k_planes[:].bitcast(I32), 0)
@@ -62,70 +66,57 @@ def tile_attend_nrm_mask_topk_kernel(tc, qT, k_words, k_scales, mk, offs, out):
         for quad in range(4):
             nc.scalar.dma_start(k_planes[32 * quad:32 * quad + 4, :].bitcast(I32), picked[8 * quad:8 * quad + 8, :].bitcast(I32))
 
-        pairs = sb.tile([P, N], U32, name="pairs", align_bytes=64)
+        q_bf = sb.tile([P, PASSES, NQ, PACK], BF16, name="q_bf", align_bytes=64)
+        q_codes = sb.tile([P, PASSES, NQ], U32, name="q_codes", align_bytes=64)
+        q_planes = sb.tile([P, PASSES, NQ], U8, name="q_planes", align_bytes=64)
+        for o in range(PASSES):
+            nc.scalar.activation(q_bf[:, o, :, :], q_raw[o][:].rearrange("p j w -> p w j"), ACT.Copy, scale=-1.0)
+
         half = N // 2
+        pairs = sb.tile([P, N], U32, name="pairs", align_bytes=64)
+        halves = pairs[:].bitcast(U16).rearrange("p (n h) -> p h n", h=PASSES)
+        k_codes = sb.tile([P, PASSES, 2 * N], U8, name="k_codes", align_bytes=64)
+        banks = [psum.tile([P, half], F32, name=f"neg_scores{h}") for h in range(2)]
+
         for h in range(2):
             nc.vector.tensor_copy(
                 pairs[:, h * half:(h + 1) * half],
                 word_pool[:].bitcast(U32).indirect(offsets[:, h * half // 16:(h + 1) * half // 16]),
             )
-        halves = pairs[:].bitcast(U16).rearrange("p (n h) -> p h n", h=PASSES)
-
-        q_bf = [
-            sb.tile([P, NQ, PACK], BF16, name=f"q_bf{o}", tag=f"q_bf{o}", align_bytes=64) for o in range(PASSES)
-        ]
-        q_codes = sb.tile([P, PASSES, NQ], U32, name="q_codes", align_bytes=64)
-        q_planes = sb.tile([P, PASSES, NQ], U8, name="q_planes", align_bytes=64)
+        for h in range(2):
+            slots = slice(h * half, (h + 1) * half)
+            for o in range(PASSES):
+                nc.vector.tensor_copy(k_codes[:, o, :].bitcast(U16)[:, slots], halves[:, o, slots])
         for o in range(PASSES):
-            nc.scalar.copy(
-                q_bf[o][:].rearrange("p (c i) j -> p c j i", i=4), q_raw[o][:].rearrange("p j (c i) -> p c j i", i=4)
-            )
-
-        mask = sb.tile([P, N], F32, name="mask", tag="q_raw0", align_bytes=64)
-        nc.sync.dma_start(mask[:], mk[0])
-
-        scores = psum.tile([P, N], F32, name="scores")
-
-        def quantise(o):
             nc.vector.quantize_mx(
                 out=q_codes[:, o, :].bitcast(FP8X4),
                 scales=q_planes[:, o, :],
-                in_=q_bf[o][:].rearrange("p w j -> p (w j)"),
+                in_=q_bf[:, o, :, :].rearrange("p w j -> p (w j)"),
             )
+        for first in range(0, N, P):
+            h, at = divmod(first, half)
+            for o in range(PASSES):
+                nc.tensor.matmul_mx(
+                    out=banks[h][:, at:at + P],
+                    lhsT=q_codes[:, o, :].bitcast(FP8X4),
+                    lhsT_scale=q_planes[:, o, :],
+                    rhs=k_codes[:, o, 2 * first:2 * (first + P)].bitcast(FP4X4),
+                    rhs_scale=k_planes[:, o * N + first:o * N + first + P],
+                    start=(o == 0),
+                    stop=(o == PASSES - 1),
+                )
 
-        def split(o, slots):
-            nc.vector.tensor_copy(k_codes[o][:].bitcast(U16)[:, slots], halves[:, o, slots])
-
-        def multiply(o):
-            nc.tensor.matmul_mx(
-                out=scores[:],
-                lhsT=q_codes[:, o, :].bitcast(FP8X4),
-                lhsT_scale=q_planes[:, o, :],
-                rhs=k_codes[o][:].bitcast(FP4X4),
-                rhs_scale=k_planes[:, o * N:(o + 1) * N],
-                start=(o == 0),
-                stop=(o == PASSES - 1),
-            )
-
-        k_codes = [sb.tile([P, 2 * N], U8, name="k_codes0", align_bytes=64)]
-        split(0, slice(0, half))
-        split(0, slice(half, N))
-        quantise(0)
-        multiply(0)
-        k_codes.append(sb.tile([P, 2 * N], U8, name="k_codes1", tag="q_bf0", align_bytes=64))
-        split(1, slice(0, N))
-        quantise(1)
-        multiply(1)
-
-        neg_max = sb.tile([P, 1], F32, name="neg_max")
-        nc.vector.tensor_reduce(neg_max[:], scores[:], AX.X, ALU.max, negate=True)
-        lifted = sb.tile([P, N], F32, name="lifted", align_bytes=64)
-        nc.vector.scalar_tensor_tensor(lifted[:], mask[:], SPAN, scores[:], ALU.mult, ALU.add)
-        shift = sb.tile([P, 1], F32, name="shift")
-        nc.scalar.activation(shift[:], neg_max[:], ACT.Copy, bias=-SPAN)
         e = sb.tile([P, N], F32, name="e", align_bytes=64)
+        sunk = sb.tile([P, N], F32, name="sunk", align_bytes=64)
+        shift = [sb.tile([P, 1], F32, name=f"shift{h}") for h in range(2)]
+        for h in range(2):
+            cols = slice(h * half, (h + 1) * half)
+            nc.vector.tensor_scalar(
+                e[:, cols], banks[h][:], -SPAN, shift[0][:] if h else None, ALU.add, ALU.min, accum_out=shift[h][:]
+            )
+            nc.vector.scalar_tensor_tensor(sunk[:, cols], mask[:, cols], -SPAN, banks[h][:], ALU.mult, ALU.add)
         total = sb.tile([P, 1], F32, name="total")
-        nc.scalar.activation(e[:], lifted[:], ACT.Exp, bias=shift[:], accum_out=total[:])
+        nc.scalar.activation(e[:], sunk[:], ACT.Exp, bias=shift[1][:], scale=-1.0, accum_out=total[:])
         inv = sb.tile([P, 1], F32, name="inv")
         nc.vector.reciprocal(inv[:], total[:])
         res = sb.tile([P, N], F32, name="res", align_bytes=64)

@@ -66,16 +66,21 @@ def tile_attend_nrm_mask_topk_kernel(tc, qT, k_words, k_scales, mk, offs, out):
         for quad in range(4):
             nc.scalar.dma_start(k_planes[32 * quad:32 * quad + 4, :].bitcast(I32), picked[8 * quad:8 * quad + 8, :].bitcast(I32))
 
-        q_bf = sb.tile([P, PASSES, NQ, PACK], BF16, name="q_bf", align_bytes=64)
+        q_bf = [
+            sb.tile([P, NQ, PACK], BF16, name=f"q_bf{o}", tag=f"q_bf{o}", align_bytes=64) for o in range(PASSES)
+        ]
         q_codes = sb.tile([P, PASSES, NQ], U32, name="q_codes", align_bytes=64)
         q_planes = sb.tile([P, PASSES, NQ], U8, name="q_planes", align_bytes=64)
-        for o in range(PASSES):
-            nc.scalar.activation(q_bf[:, o, :, :], q_raw[o][:].rearrange("p j w -> p w j"), ACT.Copy, scale=-1.0)
+
+        def uncast(o, rows):
+            return q_raw[o][:, :, rows].rearrange("p j w -> p w j")
+
+        for o, rows in ((0, slice(0, NQ)), (1, slice(0, NQ // 2))):
+            nc.scalar.activation(q_bf[o][:, rows, :], uncast(o, rows), ACT.Copy, scale=-1.0)
 
         half = N // 2
         pairs = sb.tile([P, N], U32, name="pairs", align_bytes=64)
         halves = pairs[:].bitcast(U16).rearrange("p (n h) -> p h n", h=PASSES)
-        k_codes = sb.tile([P, PASSES, 2 * N], U8, name="k_codes", align_bytes=64)
         banks = [psum.tile([P, half], F32, name=f"neg_scores{h}") for h in range(2)]
 
         for h in range(2):
@@ -83,16 +88,23 @@ def tile_attend_nrm_mask_topk_kernel(tc, qT, k_words, k_scales, mk, offs, out):
                 pairs[:, h * half:(h + 1) * half],
                 word_pool[:].bitcast(U32).indirect(offsets[:, h * half // 16:(h + 1) * half // 16]),
             )
-        for h in range(2):
-            slots = slice(h * half, (h + 1) * half)
+        k_codes = []
+
+        def part(h, tag):
+            k_codes.append(sb.tile([P, PASSES * N], U8, name=f"k_codes{h}", tag=tag, align_bytes=64))
             for o in range(PASSES):
-                nc.vector.tensor_copy(k_codes[:, o, :].bitcast(U16)[:, slots], halves[:, o, slots])
+                nc.vector.tensor_copy(k_codes[h][:, o * N:(o + 1) * N].bitcast(U16), halves[:, o, h * half:(h + 1) * half])
+
+        part(0, "k_codes0")
+        rows = slice(NQ // 2, NQ)
+        nc.vector.tensor_scalar(q_bf[1][:, rows, :], uncast(1, rows), -1.0, None, ALU.mult)
         for o in range(PASSES):
             nc.vector.quantize_mx(
                 out=q_codes[:, o, :].bitcast(FP8X4),
                 scales=q_planes[:, o, :],
-                in_=q_bf[:, o, :, :].rearrange("p w j -> p (w j)"),
+                in_=q_bf[o][:].rearrange("p w j -> p (w j)"),
             )
+        part(1, "q_bf1")
         for first in range(0, N, P):
             h, at = divmod(first, half)
             for o in range(PASSES):
@@ -100,7 +112,7 @@ def tile_attend_nrm_mask_topk_kernel(tc, qT, k_words, k_scales, mk, offs, out):
                     out=banks[h][:, at:at + P],
                     lhsT=q_codes[:, o, :].bitcast(FP8X4),
                     lhsT_scale=q_planes[:, o, :],
-                    rhs=k_codes[:, o, 2 * first:2 * (first + P)].bitcast(FP4X4),
+                    rhs=k_codes[h][:, o * N + 2 * at:o * N + 2 * (at + P)].bitcast(FP4X4),
                     rhs_scale=k_planes[:, o * N + first:o * N + first + P],
                     start=(o == 0),
                     stop=(o == PASSES - 1),

@@ -56,15 +56,11 @@ def tile_attend_nrm_mask_topk_kernel(tc, qT, k_words, k_scales, mk, offs, out):
 
         k_planes = sb.tile([P, PASSES * N], U8, name="k_planes", align_bytes=64)
         nc.vector.memset(k_planes[:].bitcast(I32), 0)
-        warm_in = sb.tile([P, 1], F32, name="warm_in")
-        warm_out = sb.tile([P, 1], F32, name="warm_out")
-        nc.vector.memset(warm_in[:], 0.0)
-        nc.scalar.activation(warm_out[:], warm_in[:], ACT.Exp)
 
         picked = sb.tile([P, N], U8, name="picked", align_bytes=64)
         nc.vector.tensor_copy(picked[:], scale_pool[:].indirect(offsets[:]))
         for quad in range(4):
-            nc.scalar.dma_start(k_planes[32 * quad:32 * quad + 4, :].bitcast(I32), picked[8 * quad:8 * quad + 8, :].bitcast(I32))
+            nc.sync.dma_start(k_planes[32 * quad:32 * quad + 4, :].bitcast(I32), picked[8 * quad:8 * quad + 8, :].bitcast(I32))
 
         q_bf = [
             sb.tile([P, NQ, PACK], BF16, name=f"q_bf{o}", tag=f"q_bf{o}", align_bytes=64) for o in range(PASSES)

@@ -43,14 +43,15 @@ def tile_attend_nrm_mask_topk_kernel(tc, qT, k_words, k_scales, mk, offs, out):
 
         word_pool = sb.tile([P, T], I32, name="word_pool", align_bytes=64)
         words = k_words[0].rearrange("p t b -> p (t b)").bitcast(I32)
-        for tokens in (slice(0, T // 4), slice(T // 4, T // 2), slice(T // 2, T)):
-            nc.sync.dma_start(word_pool[:, tokens], words[:, tokens])
+        nc.sync.dma_start(word_pool[:], words)
 
-        q_raw = [
-            sb.tile([P, PACK, NQ], F32, name=f"q_raw{o}", tag=f"q_raw{o}", align_bytes=64) for o in range(PASSES)
-        ]
+        q_raw = sb.tile([P, PASSES * K_PASS], F32, name="q_raw", align_bytes=64)
         for o in range(PASSES):
-            nc.sync.dma_start(q_raw[o][:], qT[0, o * K_PASS:(o + 1) * K_PASS, :].rearrange("(p j) w -> p j w", j=PACK))
+            nc.sync.dma_start(
+                q_raw[:, o * K_PASS:(o + 1) * K_PASS],
+                qT[0, o * K_PASS:(o + 1) * K_PASS, :].rearrange("(p j) w -> p (j w)", j=PACK),
+            )
+        q_by_row = q_raw[:].rearrange("p (o j w) -> p o w j", o=PASSES, j=PACK)
         mask = sb.tile([P, N], F32, name="mask", align_bytes=64)
         nc.sync.dma_start(mask[:], mk[0])
 
@@ -62,69 +63,85 @@ def tile_attend_nrm_mask_topk_kernel(tc, qT, k_words, k_scales, mk, offs, out):
         for quad in range(4):
             nc.sync.dma_start(k_planes[32 * quad:32 * quad + 4, :].bitcast(I32), picked[8 * quad:8 * quad + 8, :].bitcast(I32))
 
-        q_bf = [
-            sb.tile([P, NQ, PACK], BF16, name=f"q_bf{o}", tag=f"q_bf{o}", align_bytes=64) for o in range(PASSES)
-        ]
+        q_bf = sb.tile([P, PASSES * K_PASS], BF16, name="q_bf", tag="q_bf", align_bytes=64)
+        q_bf_by_row = q_bf[:].rearrange("p (o w j) -> p o w j", o=PASSES, j=PACK)
         q_codes = sb.tile([P, PASSES, NQ], U32, name="q_codes", align_bytes=64)
         q_planes = sb.tile([P, PASSES, NQ], U8, name="q_planes", align_bytes=64)
 
-        def uncast(o, rows):
-            return q_raw[o][:, :, rows].rearrange("p j w -> p w j")
-
-        for o, rows in ((0, slice(0, NQ)), (1, slice(0, NQ // 2))):
-            nc.scalar.activation(q_bf[o][:, rows, :], uncast(o, rows), ACT.Copy, scale=-1.0)
+        shared = NQ - 8
+        sign = [sb.tile([P, 1], F32, name=f"sign{i}", tag=f"late_codes{i}", align_bytes=64) for i in range(2)]
+        for one in sign:
+            nc.vector.memset(one[:], -1.0)
+        for passes, rows, scale in (
+            (0, slice(0, shared), -1.0),
+            (slice(0, PASSES), slice(shared, NQ), sign[0][:]),
+            (1, slice(NQ // 2, shared), sign[1][:]),
+        ):
+            nc.scalar.activation(q_bf_by_row[:, passes, rows, :], q_by_row[:, passes, rows, :], ACT.Copy, scale=scale)
 
         half = N // 2
         pairs = sb.tile([P, N], U32, name="pairs", align_bytes=64)
         halves = pairs[:].bitcast(U16).rearrange("p (n h) -> p h n", h=PASSES)
-        banks = [psum.tile([P, half], F32, name=f"neg_scores{h}") for h in range(2)]
+        spans = (slice(0, P), slice(P, half), slice(half, N))
+        banks = [psum.tile([P, c.stop - c.start], F32, name=f"neg_scores{i}") for i, c in enumerate(spans)]
 
         for h in range(2):
             nc.vector.tensor_copy(
                 pairs[:, h * half:(h + 1) * half],
                 word_pool[:].bitcast(U32).indirect(offsets[:, h * half // 16:(h + 1) * half // 16]),
             )
-        k_codes = []
+        early_codes = sb.tile([P, N], U8, name="early_codes", align_bytes=64)
+        mid_codes = sb.tile([P, N], U8, name="mid_codes", tag="late_codes0", align_bytes=64)
+        late_codes = sb.tile([P, PASSES * N], U8, name="late_codes", tag="late_codes1", align_bytes=64)
+        k_codes = {(0, 0): early_codes[:], (0, 1): mid_codes[:], (1, 0): late_codes[:, :N], (1, 1): late_codes[:, N:]}
 
-        def part(h, tag):
-            k_codes.append(sb.tile([P, PASSES * N], U8, name=f"k_codes{h}", tag=tag, align_bytes=64))
-            for o in range(PASSES):
-                nc.vector.tensor_copy(k_codes[h][:, o * N:(o + 1) * N].bitcast(U16), halves[:, o, h * half:(h + 1) * half])
+        def part(h, o):
+            nc.vector.tensor_copy(k_codes[h, o].bitcast(U16), halves[:, o, h * half:(h + 1) * half])
 
-        part(0, "k_codes0")
-        rows = slice(NQ // 2, NQ)
-        nc.vector.tensor_scalar(q_bf[1][:, rows, :], uncast(1, rows), -1.0, None, ALU.mult)
-        for o in range(PASSES):
+        def quantise(o):
             nc.vector.quantize_mx(
                 out=q_codes[:, o, :].bitcast(FP8X4),
                 scales=q_planes[:, o, :],
-                in_=q_bf[o][:].rearrange("p w j -> p (w j)"),
+                in_=q_bf[:, o * K_PASS:(o + 1) * K_PASS],
             )
-        part(1, "q_bf1")
-        for first in range(0, N, P):
-            h, at = divmod(first, half)
+
+        def score(group, o, bank):
+            h, at = divmod(group * P, half)
+            nc.tensor.matmul_mx(
+                out=bank,
+                lhsT=q_codes[:, o, :].bitcast(FP8X4),
+                lhsT_scale=q_planes[:, o, :],
+                rhs=k_codes[h, o][:, 2 * at:2 * (at + P)].bitcast(FP4X4),
+                rhs_scale=k_planes[:, o * N + group * P:o * N + (group + 1) * P],
+                start=(o == 0),
+                stop=(o == PASSES - 1),
+            )
+
+        part(0, 0)
+        rows = slice(0, NQ // 2)
+        nc.vector.tensor_scalar(q_bf_by_row[:, 1, rows, :], q_by_row[:, 1, rows, :], -1.0, None, ALU.mult)
+        quantise(0)
+        part(0, 1)
+        quantise(1)
+        part(1, 0)
+        part(1, 1)
+        for o in range(PASSES):
+            for group in range(2):
+                score(group, o, banks[group][:])
+        for group in range(2, 4):
             for o in range(PASSES):
-                nc.tensor.matmul_mx(
-                    out=banks[h][:, at:at + P],
-                    lhsT=q_codes[:, o, :].bitcast(FP8X4),
-                    lhsT_scale=q_planes[:, o, :],
-                    rhs=k_codes[h][:, o * N + 2 * at:o * N + 2 * (at + P)].bitcast(FP4X4),
-                    rhs_scale=k_planes[:, o * N + first:o * N + first + P],
-                    start=(o == 0),
-                    stop=(o == PASSES - 1),
-                )
+                score(group, o, banks[2][:, (group - 2) * P:(group - 1) * P])
 
         e = sb.tile([P, N], F32, name="e", align_bytes=64)
         sunk = sb.tile([P, N], F32, name="sunk", align_bytes=64)
-        shift = [sb.tile([P, 1], F32, name=f"shift{h}") for h in range(2)]
-        for h in range(2):
-            cols = slice(h * half, (h + 1) * half)
+        shift = [sb.tile([P, 1], F32, name=f"shift{i}") for i in range(len(spans))]
+        for i, cols in enumerate(spans):
             nc.vector.tensor_scalar(
-                e[:, cols], banks[h][:], -SPAN, shift[0][:] if h else None, ALU.add, ALU.min, accum_out=shift[h][:]
+                e[:, cols], banks[i][:], -SPAN, shift[i - 1][:] if i else None, ALU.add, ALU.min, accum_out=shift[i][:]
             )
-            nc.vector.scalar_tensor_tensor(sunk[:, cols], mask[:, cols], -SPAN, banks[h][:], ALU.mult, ALU.add)
+            nc.vector.scalar_tensor_tensor(sunk[:, cols], mask[:, cols], -SPAN, banks[i][:], ALU.mult, ALU.add)
         total = sb.tile([P, 1], F32, name="total")
-        nc.scalar.activation(e[:], sunk[:], ACT.Exp, bias=shift[1][:], scale=-1.0, accum_out=total[:])
+        nc.scalar.activation(e[:], sunk[:], ACT.Exp, bias=shift[-1][:], scale=-1.0, accum_out=total[:])
         inv = sb.tile([P, 1], F32, name="inv")
         nc.vector.reciprocal(inv[:], total[:])
         res = sb.tile([P, N], F32, name="res", align_bytes=64)

@@ -58,10 +58,15 @@ def tile_attend_nrm_mask_topk_kernel(tc, qT, k_words, k_scales, mk, offs, out):
         k_planes = sb.tile([P, PASSES * N], U8, name="k_planes", align_bytes=64)
         nc.vector.memset(k_planes[:].bitcast(I32), 0)
 
+        sign = [sb.tile([P, 1], F32, name=f"sign{i}", tag=f"late_codes{i}", align_bytes=64) for i in range(2)]
+        nc.vector.memset(sign[1][:], -1.0)
+        nc.scalar.activation(sign[0][:], sign[1][:], ACT.Copy)
+
         picked = sb.tile([P, N], U8, name="picked", align_bytes=64)
         nc.vector.tensor_copy(picked[:], scale_pool[:].indirect(offsets[:]))
         for quad in range(4):
-            nc.sync.dma_start(k_planes[32 * quad:32 * quad + 4, :].bitcast(I32), picked[8 * quad:8 * quad + 8, :].bitcast(I32))
+            queue = nc.sync if quad < 2 else nc.scalar
+            queue.dma_start(k_planes[32 * quad:32 * quad + 4, :].bitcast(I32), picked[8 * quad:8 * quad + 8, :].bitcast(I32))
 
         q_bf = sb.tile([P, PASSES * K_PASS], BF16, name="q_bf", tag="q_bf", align_bytes=64)
         q_bf_by_row = q_bf[:].rearrange("p (o w j) -> p o w j", o=PASSES, j=PACK)
@@ -69,9 +74,6 @@ def tile_attend_nrm_mask_topk_kernel(tc, qT, k_words, k_scales, mk, offs, out):
         q_planes = sb.tile([P, PASSES, NQ], U8, name="q_planes", align_bytes=64)
 
         shared = NQ - 8
-        sign = [sb.tile([P, 1], F32, name=f"sign{i}", tag=f"late_codes{i}", align_bytes=64) for i in range(2)]
-        for one in sign:
-            nc.vector.memset(one[:], -1.0)
         for passes, rows, scale in (
             (0, slice(0, shared), -1.0),
             (slice(0, PASSES), slice(shared, NQ), sign[0][:]),

@@ -84,7 +84,7 @@ def tile_attend_nrm_mask_topk_kernel(tc, qT, k_words, k_scales, mk, offs, out):
         half = N // 2
         pairs = sb.tile([P, N], U32, name="pairs", align_bytes=64)
         halves = pairs[:].bitcast(U16).rearrange("p (n h) -> p h n", h=PASSES)
-        spans = (slice(0, P), slice(P, half), slice(half, N))
+        spans = [slice(first, first + P) for first in range(0, N, P)]
         banks = [psum.tile([P, c.stop - c.start], F32, name=f"neg_scores{i}") for i, c in enumerate(spans)]
 
         for h in range(2):
@@ -132,22 +132,27 @@ def tile_attend_nrm_mask_topk_kernel(tc, qT, k_words, k_scales, mk, offs, out):
                 score(group, o, banks[group][:])
         for group in range(2, 4):
             for o in range(PASSES):
-                score(group, o, banks[2][:, (group - 2) * P:(group - 1) * P])
+                score(group, o, banks[group][:])
 
         e = sb.tile([P, N], F32, name="e", align_bytes=64)
         sunk = sb.tile([P, N], F32, name="sunk", align_bytes=64)
-        shift = [sb.tile([P, 1], F32, name=f"shift{i}") for i in range(len(spans))]
+        lows = sb.tile([P, len(spans)], F32, name="lows")
         for i, cols in enumerate(spans):
-            nc.vector.tensor_scalar(
-                e[:, cols], banks[i][:], -SPAN, shift[i - 1][:] if i else None, ALU.add, ALU.min, accum_out=shift[i][:]
-            )
+            nc.vector.tensor_reduce(lows[:, i:i + 1], banks[i][:], AX.X, ALU.min)
             nc.vector.scalar_tensor_tensor(sunk[:, cols], mask[:, cols], -SPAN, banks[i][:], ALU.mult, ALU.add)
+        low = sb.tile([P, 1], F32, name="low")
+        lowered = sb.tile([P, len(spans)], F32, name="lowered")
+        nc.vector.tensor_scalar(lowered[:], lows[:], -SPAN, None, ALU.add, ALU.min, accum_out=low[:])
         total = sb.tile([P, 1], F32, name="total")
-        nc.scalar.activation(e[:], sunk[:], ACT.Exp, bias=shift[-1][:], scale=-1.0, accum_out=total[:])
+        nc.scalar.activation(e[:], sunk[:], ACT.Exp, bias=low[:], scale=-1.0, accum_out=total[:])
         inv = sb.tile([P, 1], F32, name="inv")
         nc.vector.reciprocal(inv[:], total[:])
         res = sb.tile([P, N], F32, name="res", align_bytes=64)
-        nc.vector.tensor_scalar(res[:, :half], e[:, :half], inv[:], None, ALU.mult)
-        nc.sync.dma_start(out[0, :, :half], res[:, :half])
-        nc.scalar.activation(res[:, half:], e[:, half:], ACT.Copy, scale=inv[:])
-        nc.scalar.dma_start(out[0, :, half:], res[:, half:])
+        for first in range(0, N, P):
+            cols = slice(first, first + P)
+            if first < half:
+                nc.vector.tensor_scalar(res[:, cols], e[:, cols], inv[:], None, ALU.mult)
+                nc.sync.dma_start(out[0, :, cols], res[:, cols])
+            else:
+                nc.scalar.activation(res[:, cols], e[:, cols], ACT.Copy, scale=inv[:])
+                nc.scalar.dma_start(out[0, :, cols], res[:, cols])

@@ -137,9 +137,12 @@ def tile_attend_nrm_mask_topk_kernel(tc, qT, k_words, k_scales, mk, offs, out):
         e = sb.tile([P, N], F32, name="e", align_bytes=64)
         sunk = sb.tile([P, N], F32, name="sunk", align_bytes=64)
         lows = sb.tile([P, len(spans)], F32, name="lows")
-        for i, cols in enumerate(spans):
-            nc.vector.tensor_reduce(lows[:, i:i + 1], banks[i][:], AX.X, ALU.min)
-            nc.vector.scalar_tensor_tensor(sunk[:, cols], mask[:, cols], -SPAN, banks[i][:], ALU.mult, ALU.add)
+        for together in ((0,), (1,), (2, 3)):
+            for i in together:
+                nc.vector.tensor_reduce(lows[:, i:i + 1], banks[i][:], AX.X, ALU.min)
+            for i in together:
+                cols = spans[i]
+                nc.vector.scalar_tensor_tensor(sunk[:, cols], mask[:, cols], -SPAN, banks[i][:], ALU.mult, ALU.add)
         low = sb.tile([P, 1], F32, name="low")
         lowered = sb.tile([P, len(spans)], F32, name="lowered")
         nc.vector.tensor_scalar(lowered[:], lows[:], -SPAN, None, ALU.add, ALU.min, accum_out=low[:])
@@ -148,11 +151,7 @@ def tile_attend_nrm_mask_topk_kernel(tc, qT, k_words, k_scales, mk, offs, out):
         inv = sb.tile([P, 1], F32, name="inv")
         nc.vector.reciprocal(inv[:], total[:])
         res = sb.tile([P, N], F32, name="res", align_bytes=64)
-        for first in range(0, N, P):
-            cols = slice(first, first + P)
-            if first < half:
-                nc.vector.tensor_scalar(res[:, cols], e[:, cols], inv[:], None, ALU.mult)
-                nc.sync.dma_start(out[0, :, cols], res[:, cols])
-            else:
-                nc.scalar.activation(res[:, cols], e[:, cols], ACT.Copy, scale=inv[:])
-                nc.scalar.dma_start(out[0, :, cols], res[:, cols])
+        nc.vector.tensor_scalar(res[:, :half], e[:, :half], inv[:], None, ALU.mult)
+        nc.sync.dma_start(out[0, :, :half], res[:, :half])
+        nc.scalar.activation(res[:, half:], e[:, half:], ACT.Copy, scale=inv[:])
+        nc.scalar.dma_start(out[0, :, half:], res[:, half:])

@@ -23,6 +23,8 @@ N = 512
 T = 2048
 
 SPAN = 128.0
+ROWS_ON_VECTOR = 64
+SCALED_ON_VECTOR = 352
 
 FLOPS = 2 * NQ * N * PASSES * K_PASS
 
@@ -73,13 +75,18 @@ def tile_attend_nrm_mask_topk_kernel(tc, qT, k_words, k_scales, mk, offs, out):
         q_codes = sb.tile([P, PASSES, NQ], U32, name="q_codes", align_bytes=64)
         q_planes = sb.tile([P, PASSES, NQ], U8, name="q_planes", align_bytes=64)
 
+        def walk(by_row, passes, rows):
+            if isinstance(passes, slice):
+                return by_row[:, passes, rows, :]
+            return by_row[:, passes, rows, :].rearrange("p (c i) j -> p c j i", i=4)
+
         shared = NQ - 8
         for passes, rows, scale in (
             (0, slice(0, shared), -1.0),
             (slice(0, PASSES), slice(shared, NQ), sign[0][:]),
-            (1, slice(NQ // 2, shared), sign[1][:]),
+            (1, slice(ROWS_ON_VECTOR, shared), sign[1][:]),
         ):
-            nc.scalar.activation(q_bf_by_row[:, passes, rows, :], q_by_row[:, passes, rows, :], ACT.Copy, scale=scale)
+            nc.scalar.activation(walk(q_bf_by_row, passes, rows), walk(q_by_row, passes, rows), ACT.Copy, scale=scale)
 
         half = N // 2
         pairs = sb.tile([P, N], U32, name="pairs", align_bytes=64)
@@ -120,8 +127,8 @@ def tile_attend_nrm_mask_topk_kernel(tc, qT, k_words, k_scales, mk, offs, out):
             )
 
         part(0, 0)
-        rows = slice(0, NQ // 2)
-        nc.vector.tensor_scalar(q_bf_by_row[:, 1, rows, :], q_by_row[:, 1, rows, :], -1.0, None, ALU.mult)
+        rows = slice(0, ROWS_ON_VECTOR)
+        nc.vector.tensor_scalar(walk(q_bf_by_row, 1, rows), walk(q_by_row, 1, rows), -1.0, None, ALU.mult)
         quantise(0)
         part(0, 1)
         quantise(1)
@@ -153,5 +160,6 @@ def tile_attend_nrm_mask_topk_kernel(tc, qT, k_words, k_scales, mk, offs, out):
         res = sb.tile([P, N], F32, name="res", align_bytes=64)
         nc.vector.tensor_scalar(res[:, :half], e[:, :half], inv[:], None, ALU.mult)
         nc.sync.dma_start(out[0, :, :half], res[:, :half])
-        nc.scalar.activation(res[:, half:], e[:, half:], ACT.Copy, scale=inv[:])
+        nc.vector.tensor_scalar(res[:, half:SCALED_ON_VECTOR], e[:, half:SCALED_ON_VECTOR], inv[:], None, ALU.mult)
+        nc.scalar.activation(res[:, SCALED_ON_VECTOR:], e[:, SCALED_ON_VECTOR:], ACT.Copy, scale=inv[:])
         nc.scalar.dma_start(out[0, :, half:], res[:, half:])

@@ -67,7 +67,7 @@ def tile_attend_nrm_mask_topk_kernel(tc, qT, k_words, k_scales, mk, offs, out):
         picked = sb.tile([P, N], U8, name="picked", align_bytes=64)
         nc.vector.tensor_copy(picked[:], scale_pool[:].indirect(offsets[:]))
         for quad in range(4):
-            queue = nc.sync if quad < 2 else nc.scalar
+            queue = nc.sync if quad % 2 == 0 else nc.scalar
             queue.dma_start(k_planes[32 * quad:32 * quad + 4, :].bitcast(I32), picked[8 * quad:8 * quad + 8, :].bitcast(I32))
 
         q_bf = sb.tile([P, PASSES * K_PASS], BF16, name="q_bf", tag="q_bf", align_bytes=64)

@@ -21,9 +21,11 @@ K_PASS = P * PACK
 NQ = 128
 N = 512
 T = 2048
+GROUPS = N // P
 
-SPAN = 128.0
-ROWS_ON_VECTOR = 64
+SPAN = 256.0
+ROWS_ON_VECTOR = 48
+ROWS_OF_BOTH = 8
 SCALED_ON_VECTOR = 352
 
 FLOPS = 2 * NQ * N * PASSES * K_PASS
@@ -45,116 +47,104 @@ def tile_attend_nrm_mask_topk_kernel(tc, qT, k_words, k_scales, mk, offs, out):
 
         word_pool = sb.tile([P, T], I32, name="word_pool", align_bytes=64)
         words = k_words[0].rearrange("p t b -> p (t b)").bitcast(I32)
-        nc.sync.dma_start(word_pool[:], words)
+        for first in range(2):
+            nc.sync.dma_start(word_pool[first:P:2, :], words[first:P:2, :])
 
-        q_raw = sb.tile([P, PASSES * K_PASS], F32, name="q_raw", align_bytes=64)
+        q_raw = sb.tile([P, PASSES, K_PASS], F32, name="q_raw", align_bytes=64)
         for o in range(PASSES):
-            nc.sync.dma_start(
-                q_raw[:, o * K_PASS:(o + 1) * K_PASS],
-                qT[0, o * K_PASS:(o + 1) * K_PASS, :].rearrange("(p j) w -> p (j w)", j=PACK),
-            )
-        q_by_row = q_raw[:].rearrange("p (o j w) -> p o w j", o=PASSES, j=PACK)
+            nc.sync.dma_start(q_raw[:, o, :], qT[0, o * K_PASS:(o + 1) * K_PASS, :].rearrange("(p j) w -> p (j w)", j=PACK))
         mask = sb.tile([P, N], F32, name="mask", align_bytes=64)
         nc.sync.dma_start(mask[:], mk[0])
 
         k_planes = sb.tile([P, PASSES * N], U8, name="k_planes", align_bytes=64)
         nc.vector.memset(k_planes[:].bitcast(I32), 0)
 
-        sign = [sb.tile([P, 1], F32, name=f"sign{i}", tag=f"late_codes{i}", align_bytes=64) for i in range(2)]
-        nc.vector.memset(sign[1][:], -1.0)
-        nc.scalar.activation(sign[0][:], sign[1][:], ACT.Copy)
+        span = sb.tile([P, 1], F32, name="span")
+        nc.vector.memset(span[:], SPAN)
+        unit = sb.tile([P, 1], F32, name="unit", tag="mid_codes", align_bytes=64)
+        nc.scalar.activation(unit[:], span[:], ACT.Copy, scale=1.0 / SPAN ** 2)
 
         picked = sb.tile([P, N], U8, name="picked", align_bytes=64)
         nc.vector.tensor_copy(picked[:], scale_pool[:].indirect(offsets[:]))
         for quad in range(4):
-            queue = nc.sync if quad % 2 == 0 else nc.scalar
-            queue.dma_start(k_planes[32 * quad:32 * quad + 4, :].bitcast(I32), picked[8 * quad:8 * quad + 8, :].bitcast(I32))
+            nc.scalar.dma_start(k_planes[32 * quad:32 * quad + 4, :].bitcast(I32), picked[8 * quad:8 * quad + 8, :].bitcast(I32))
 
-        q_bf = sb.tile([P, PASSES * K_PASS], BF16, name="q_bf", tag="q_bf", align_bytes=64)
-        q_bf_by_row = q_bf[:].rearrange("p (o w j) -> p o w j", o=PASSES, j=PACK)
+        q_bf = sb.tile([P, PASSES, K_PASS], BF16, name="q_bf", align_bytes=64)
         q_codes = sb.tile([P, PASSES, NQ], U32, name="q_codes", align_bytes=64)
         q_planes = sb.tile([P, PASSES, NQ], U8, name="q_planes", align_bytes=64)
 
-        def walk(by_row, passes, rows):
-            if isinstance(passes, slice):
-                return by_row[:, passes, rows, :]
-            return by_row[:, passes, rows, :].rearrange("p (c i) j -> p c j i", i=4)
+        q_bf_by_row = q_bf[:].rearrange("p o (w j) -> p o w j", j=PACK)
+        q_by_row = q_raw[:].rearrange("p o (j w) -> p o w j", j=PACK)
 
-        shared = NQ - 8
-        for passes, rows, scale in (
-            (0, slice(0, shared), -1.0),
-            (slice(0, PASSES), slice(shared, NQ), sign[0][:]),
-            (1, slice(ROWS_ON_VECTOR, shared), sign[1][:]),
-        ):
-            nc.scalar.activation(walk(q_bf_by_row, passes, rows), walk(q_by_row, passes, rows), ACT.Copy, scale=scale)
+        def cast_views(o, rows):
+            return [view[:, o, rows, :].rearrange("p (c i) j -> p c j i", i=4) for view in (q_bf_by_row, q_by_row)]
+
+        shared = NQ - ROWS_OF_BOTH
+        nc.scalar.activation(*cast_views(0, slice(0, shared)), ACT.Copy, scale=1.0 / SPAN)
+        nc.scalar.activation(q_bf_by_row[:, :, shared:, :], q_by_row[:, :, shared:, :], ACT.Copy, scale=unit[:])
+        nc.scalar.activation(*cast_views(1, slice(ROWS_ON_VECTOR, shared)), ACT.Copy, scale=1.0 / SPAN)
 
         half = N // 2
         pairs = sb.tile([P, N], U32, name="pairs", align_bytes=64)
         halves = pairs[:].bitcast(U16).rearrange("p (n h) -> p h n", h=PASSES)
-        spans = [slice(first, first + P) for first in range(0, N, P)]
-        banks = [psum.tile([P, c.stop - c.start], F32, name=f"neg_scores{i}") for i, c in enumerate(spans)]
-
         for h in range(2):
             nc.vector.tensor_copy(
                 pairs[:, h * half:(h + 1) * half],
                 word_pool[:].bitcast(U32).indirect(offsets[:, h * half // 16:(h + 1) * half // 16]),
             )
-        early_codes = sb.tile([P, N], U8, name="early_codes", align_bytes=64)
-        mid_codes = sb.tile([P, N], U8, name="mid_codes", tag="late_codes0", align_bytes=64)
-        late_codes = sb.tile([P, PASSES * N], U8, name="late_codes", tag="late_codes1", align_bytes=64)
-        k_codes = {(0, 0): early_codes[:], (0, 1): mid_codes[:], (1, 0): late_codes[:, :N], (1, 1): late_codes[:, N:]}
 
-        def part(h, o):
-            nc.vector.tensor_copy(k_codes[h, o].bitcast(U16), halves[:, o, h * half:(h + 1) * half])
+        k_codes = {}
+
+        def part(room, o, groups):
+            width = len(groups) * P
+            nc.vector.tensor_copy(room, halves[:, o, groups[0] * P:groups[0] * P + width])
+            for i, group in enumerate(groups):
+                k_codes[group, o] = room[:, i * P:(i + 1) * P]
 
         def quantise(o):
-            nc.vector.quantize_mx(
-                out=q_codes[:, o, :].bitcast(FP8X4),
-                scales=q_planes[:, o, :],
-                in_=q_bf[:, o * K_PASS:(o + 1) * K_PASS],
-            )
+            nc.vector.quantize_mx(out=q_codes[:, o, :].bitcast(FP8X4), scales=q_planes[:, o, :], in_=q_bf[:, o, :])
 
-        def score(group, o, bank):
-            h, at = divmod(group * P, half)
+        banks = [psum.tile([P, P], F32, name=f"scores{group}") for group in range(GROUPS)]
+
+        def score(group, o):
             nc.tensor.matmul_mx(
-                out=bank,
+                out=banks[group][:],
                 lhsT=q_codes[:, o, :].bitcast(FP8X4),
                 lhsT_scale=q_planes[:, o, :],
-                rhs=k_codes[h, o][:, 2 * at:2 * (at + P)].bitcast(FP4X4),
+                rhs=k_codes[group, o].bitcast(FP4X4),
                 rhs_scale=k_planes[:, o * N + group * P:o * N + (group + 1) * P],
                 start=(o == 0),
                 stop=(o == PASSES - 1),
             )
 
-        part(0, 0)
-        rows = slice(0, ROWS_ON_VECTOR)
-        nc.vector.tensor_scalar(walk(q_bf_by_row, 1, rows), walk(q_by_row, 1, rows), -1.0, None, ALU.mult)
+        early_codes = sb.tile([P, half], U16, name="early_codes", align_bytes=64)
+        part(early_codes[:], 0, (0, 1))
+        nc.vector.tensor_scalar(*cast_views(1, slice(0, ROWS_ON_VECTOR)), 1.0 / SPAN, None, ALU.mult)
         quantise(0)
-        part(0, 1)
+        mid_codes = sb.tile([P, half], U16, name="mid_codes", tag="mid_codes", align_bytes=64)
+        part(mid_codes[:, :P], 1, (0,))
+        part(mid_codes[:, P:], 1, (1,))
         quantise(1)
-        part(1, 0)
-        part(1, 1)
-        for o in range(PASSES):
-            for group in range(2):
-                score(group, o, banks[group][:])
-        for group in range(2, 4):
-            for o in range(PASSES):
-                score(group, o, banks[group][:])
+        late_codes = sb.tile([P, N], U16, name="late_codes", tag="q_raw", align_bytes=64)
+        for i, (group, o) in enumerate(((2, 0), (2, 1), (3, 0), (3, 1))):
+            part(late_codes[:, i * P:(i + 1) * P], o, (group,))
+        for group, o in ((0, 0), (1, 0), (0, 1), (1, 1), (2, 0), (2, 1), (3, 0), (3, 1)):
+            score(group, o)
 
-        e = sb.tile([P, N], F32, name="e", align_bytes=64)
         sunk = sb.tile([P, N], F32, name="sunk", align_bytes=64)
-        lows = sb.tile([P, len(spans)], F32, name="lows")
+        tops = sb.tile([P, GROUPS], F32, name="tops")
         for together in ((0,), (1,), (2, 3)):
-            for i in together:
-                nc.vector.tensor_reduce(lows[:, i:i + 1], banks[i][:], AX.X, ALU.min)
-            for i in together:
-                cols = spans[i]
-                nc.vector.scalar_tensor_tensor(sunk[:, cols], mask[:, cols], -SPAN, banks[i][:], ALU.mult, ALU.add)
-        low = sb.tile([P, 1], F32, name="low")
-        lowered = sb.tile([P, len(spans)], F32, name="lowered")
-        nc.vector.tensor_scalar(lowered[:], lows[:], -SPAN, None, ALU.add, ALU.min, accum_out=low[:])
+            for group in together:
+                nc.vector.tensor_reduce(tops[:, group:group + 1], banks[group][:], AX.X, ALU.max)
+            for group in together:
+                cols = slice(group * P, (group + 1) * P)
+                nc.vector.scalar_tensor_tensor(sunk[:, cols], mask[:, cols], 1.0, banks[group][:], ALU.subtract, ALU.add)
+        shift = sb.tile([P, 1], F32, name="shift")
+        shifts = sb.tile([P, GROUPS], F32, name="shifts")
+        nc.vector.tensor_scalar(shifts[:], tops[:], -SPAN, None, ALU.mult, ALU.min, accum_out=shift[:])
+        e = sb.tile([P, N], F32, name="e", align_bytes=64)
         total = sb.tile([P, 1], F32, name="total")
-        nc.scalar.activation(e[:], sunk[:], ACT.Exp, bias=low[:], scale=-1.0, accum_out=total[:])
+        nc.scalar.activation(e[:], sunk[:], ACT.Exp, bias=shift[:], scale=SPAN, accum_out=total[:])
         inv = sb.tile([P, 1], F32, name="inv")
         nc.vector.reciprocal(inv[:], total[:])
         res = sb.tile([P, N], F32, name="res", align_bytes=64)

@@ -47,8 +47,7 @@ def tile_attend_nrm_mask_topk_kernel(tc, qT, k_words, k_scales, mk, offs, out):
 
         word_pool = sb.tile([P, T], I32, name="word_pool", align_bytes=64)
         words = k_words[0].rearrange("p t b -> p (t b)").bitcast(I32)
-        for first in range(2):
-            nc.sync.dma_start(word_pool[first:P:2, :], words[first:P:2, :])
+        nc.sync.dma_start(word_pool[:], words)
 
         q_raw = sb.tile([P, PASSES, K_PASS], F32, name="q_raw", align_bytes=64)
         for o in range(PASSES):
@@ -67,7 +66,8 @@ def tile_attend_nrm_mask_topk_kernel(tc, qT, k_words, k_scales, mk, offs, out):
         picked = sb.tile([P, N], U8, name="picked", align_bytes=64)
         nc.vector.tensor_copy(picked[:], scale_pool[:].indirect(offsets[:]))
         for quad in range(4):
-            nc.scalar.dma_start(k_planes[32 * quad:32 * quad + 4, :].bitcast(I32), picked[8 * quad:8 * quad + 8, :].bitcast(I32))
+            queue = nc.sync if quad % 2 == 0 else nc.scalar
+            queue.dma_start(k_planes[32 * quad:32 * quad + 4, :].bitcast(I32), picked[8 * quad:8 * quad + 8, :].bitcast(I32))
 
         q_bf = sb.tile([P, PASSES, K_PASS], BF16, name="q_bf", align_bytes=64)
         q_codes = sb.tile([P, PASSES, NQ], U32, name="q_codes", align_bytes=64)
@@ -117,13 +117,13 @@ def tile_attend_nrm_mask_topk_kernel(tc, qT, k_words, k_scales, mk, offs, out):
                 stop=(o == PASSES - 1),
             )
 
-        early_codes = sb.tile([P, half], U16, name="early_codes", align_bytes=64)
-        part(early_codes[:], 0, (0, 1))
+        early_codes = sb.tile([P, P], U16, name="early_codes", align_bytes=64)
+        part(early_codes[:], 0, (0,))
         nc.vector.tensor_scalar(*cast_views(1, slice(0, ROWS_ON_VECTOR)), 1.0 / SPAN, None, ALU.mult)
         quantise(0)
-        mid_codes = sb.tile([P, half], U16, name="mid_codes", tag="mid_codes", align_bytes=64)
-        part(mid_codes[:, :P], 1, (0,))
-        part(mid_codes[:, P:], 1, (1,))
+        mid_codes = sb.tile([P, 3 * P], U16, name="mid_codes", tag="mid_codes", align_bytes=64)
+        part(mid_codes[:, :P], 0, (1,))
+        part(mid_codes[:, P:], 1, (0, 1))
         quantise(1)
         late_codes = sb.tile([P, N], U16, name="late_codes", tag="q_raw", align_bytes=64)
         for i, (group, o) in enumerate(((2, 0), (2, 1), (3, 0), (3, 1))):

@@ -61,7 +61,9 @@ def tile_attend_nrm_mask_topk_kernel(tc, qT, k_words, k_scales, mk, offs, out):
         span = sb.tile([P, 1], F32, name="span")
         nc.vector.memset(span[:], SPAN)
         unit = sb.tile([P, 1], F32, name="unit", tag="mid_codes", align_bytes=64)
-        nc.scalar.activation(unit[:], span[:], ACT.Copy, scale=1.0 / SPAN ** 2)
+        nc.vector.reciprocal(unit[:], span[:])
+        last_unit = sb.tile([P, 1], F32, name="last_unit")
+        nc.scalar.activation(last_unit[:], unit[:], ACT.Copy)
 
         picked = sb.tile([P, N], U8, name="picked", align_bytes=64)
         nc.vector.tensor_copy(picked[:], scale_pool[:].indirect(offsets[:]))
@@ -82,7 +84,7 @@ def tile_attend_nrm_mask_topk_kernel(tc, qT, k_words, k_scales, mk, offs, out):
         shared = NQ - ROWS_OF_BOTH
         nc.scalar.activation(*cast_views(0, slice(0, shared)), ACT.Copy, scale=1.0 / SPAN)
         nc.scalar.activation(q_bf_by_row[:, :, shared:, :], q_by_row[:, :, shared:, :], ACT.Copy, scale=unit[:])
-        nc.scalar.activation(*cast_views(1, slice(ROWS_ON_VECTOR, shared)), ACT.Copy, scale=1.0 / SPAN)
+        nc.scalar.activation(*cast_views(1, slice(ROWS_ON_VECTOR, shared)), ACT.Copy, scale=last_unit[:])
 
         half = N // 2
         pairs = sb.tile([P, N], U32, name="pairs", align_bytes=64)

@@ -53,7 +53,7 @@ def tile_attend_nrm_mask_topk_kernel(tc, qT, k_words, k_scales, mk, offs, out):
         for o in range(PASSES):
             nc.sync.dma_start(q_raw[:, o, :], qT[0, o * K_PASS:(o + 1) * K_PASS, :].rearrange("(p j) w -> p (j w)", j=PACK))
         mask = sb.tile([P, N], F32, name="mask", align_bytes=64)
-        nc.sync.dma_start(mask[:], mk[0])
+        nc.sync.dma_start(mask[:, :N // 2], mk[0, :, :N // 2])
 
         k_planes = sb.tile([P, PASSES * N], U8, name="k_planes", align_bytes=64)
         nc.vector.memset(k_planes[:].bitcast(I32), 0)
@@ -70,6 +70,8 @@ def tile_attend_nrm_mask_topk_kernel(tc, qT, k_words, k_scales, mk, offs, out):
         for quad in range(4):
             queue = nc.sync if quad % 2 == 0 else nc.scalar
             queue.dma_start(k_planes[32 * quad:32 * quad + 4, :].bitcast(I32), picked[8 * quad:8 * quad + 8, :].bitcast(I32))
+        for first in range(N // 2, N, P):
+            nc.sync.dma_start(mask[:, first:first + P], mk[0, :, first:first + P])
 
         q_bf = sb.tile([P, PASSES, K_PASS], BF16, name="q_bf", align_bytes=64)
         q_codes = sb.tile([P, PASSES, NQ], U32, name="q_codes", align_bytes=64)

@@ -25,7 +25,7 @@ GROUPS = N // P
 
 SPAN = 256.0
 ROWS_ON_VECTOR = 48
-ROWS_OF_BOTH = 8
+ROWS_FIRST = 96
 SCALED_ON_VECTOR = 352
 
 FLOPS = 2 * NQ * N * PASSES * K_PASS
@@ -49,9 +49,9 @@ def tile_attend_nrm_mask_topk_kernel(tc, qT, k_words, k_scales, mk, offs, out):
         words = k_words[0].rearrange("p t b -> p (t b)").bitcast(I32)
         nc.sync.dma_start(word_pool[:], words)
 
-        q_raw = sb.tile([P, PASSES, K_PASS], F32, name="q_raw", align_bytes=64)
+        q_raw = [sb.tile([P, K_PASS], F32, name=f"q_raw{o}", align_bytes=64) for o in range(PASSES)]
         for o in range(PASSES):
-            nc.sync.dma_start(q_raw[:, o, :], qT[0, o * K_PASS:(o + 1) * K_PASS, :].rearrange("(p j) w -> p (j w)", j=PACK))
+            nc.sync.dma_start(q_raw[o][:], qT[0, o * K_PASS:(o + 1) * K_PASS, :].rearrange("(p j) w -> p (j w)", j=PACK))
         mask = sb.tile([P, N], F32, name="mask", align_bytes=64)
         nc.sync.dma_start(mask[:, :N // 2], mk[0, :, :N // 2])
 
@@ -60,7 +60,7 @@ def tile_attend_nrm_mask_topk_kernel(tc, qT, k_words, k_scales, mk, offs, out):
 
         span = sb.tile([P, 1], F32, name="span")
         nc.vector.memset(span[:], SPAN)
-        unit = sb.tile([P, 1], F32, name="unit", tag="mid_codes", align_bytes=64)
+        unit = sb.tile([P, 1], F32, name="unit", tag="early_codes", align_bytes=64)
         nc.vector.reciprocal(unit[:], span[:])
         last_unit = sb.tile([P, 1], F32, name="last_unit")
         nc.scalar.activation(last_unit[:], unit[:], ACT.Copy)
@@ -77,16 +77,14 @@ def tile_attend_nrm_mask_topk_kernel(tc, qT, k_words, k_scales, mk, offs, out):
         q_codes = sb.tile([P, PASSES, NQ], U32, name="q_codes", align_bytes=64)
         q_planes = sb.tile([P, PASSES, NQ], U8, name="q_planes", align_bytes=64)
 
-        q_bf_by_row = q_bf[:].rearrange("p o (w j) -> p o w j", j=PACK)
-        q_by_row = q_raw[:].rearrange("p o (j w) -> p o w j", j=PACK)
-
         def cast_views(o, rows):
-            return [view[:, o, rows, :].rearrange("p (c i) j -> p c j i", i=4) for view in (q_bf_by_row, q_by_row)]
+            dst = q_bf[:, o, :].rearrange("p (w j) -> p w j", j=PACK)[:, rows, :]
+            src = q_raw[o][:].rearrange("p (j w) -> p w j", j=PACK)[:, rows, :]
+            return [view.rearrange("p (c i) j -> p c j i", i=4) for view in (dst, src)]
 
-        shared = NQ - ROWS_OF_BOTH
-        nc.scalar.activation(*cast_views(0, slice(0, shared)), ACT.Copy, scale=1.0 / SPAN)
-        nc.scalar.activation(q_bf_by_row[:, :, shared:, :], q_by_row[:, :, shared:, :], ACT.Copy, scale=unit[:])
-        nc.scalar.activation(*cast_views(1, slice(ROWS_ON_VECTOR, shared)), ACT.Copy, scale=last_unit[:])
+        nc.scalar.activation(*cast_views(0, slice(0, ROWS_FIRST)), ACT.Copy, scale=unit[:])
+        nc.scalar.activation(*cast_views(0, slice(ROWS_FIRST, NQ)), ACT.Copy, scale=last_unit[:])
+        nc.scalar.activation(*cast_views(1, slice(ROWS_ON_VECTOR, NQ)), ACT.Copy, scale=1.0 / SPAN)
 
         half = N // 2
         pairs = sb.tile([P, N], U32, name="pairs", align_bytes=64)
@@ -121,15 +119,15 @@ def tile_attend_nrm_mask_topk_kernel(tc, qT, k_words, k_scales, mk, offs, out):
                 stop=(o == PASSES - 1),
             )
 
-        early_codes = sb.tile([P, P], U16, name="early_codes", align_bytes=64)
-        part(early_codes[:], 0, (0,))
-        nc.vector.tensor_scalar(*cast_views(1, slice(0, ROWS_ON_VECTOR)), 1.0 / SPAN, None, ALU.mult)
+        early_codes = sb.tile([P, half], U16, name="early_codes", align_bytes=64)
+        part(early_codes[:], 0, (0, 1))
         quantise(0)
-        mid_codes = sb.tile([P, 3 * P], U16, name="mid_codes", tag="mid_codes", align_bytes=64)
-        part(mid_codes[:, :P], 0, (1,))
-        part(mid_codes[:, P:], 1, (0, 1))
+        nc.vector.tensor_scalar(*cast_views(1, slice(0, ROWS_ON_VECTOR)), 1.0 / SPAN, None, ALU.mult)
+        mid_codes = sb.tile([P, half], U16, name="mid_codes", tag="q_raw0", align_bytes=64)
+        part(mid_codes[:, :P], 1, (0,))
+        part(mid_codes[:, P:], 1, (1,))
         quantise(1)
-        late_codes = sb.tile([P, N], U16, name="late_codes", tag="q_raw", align_bytes=64)
+        late_codes = sb.tile([P, N], U16, name="late_codes", tag="q_raw1", align_bytes=64)
         for i, (group, o) in enumerate(((2, 0), (2, 1), (3, 0), (3, 1))):
             part(late_codes[:, i * P:(i + 1) * P], o, (group,))
         for group, o in ((0, 0), (1, 0), (0, 1), (1, 1), (2, 0), (2, 1), (3, 0), (3, 1)):

from contextlib import ExitStack

import concourse.mybir as mybir

F32 = mybir.dt.float32
BF16 = mybir.dt.bfloat16
I32 = mybir.dt.int32
U32 = mybir.dt.uint32
U16 = mybir.dt.uint16
U8 = mybir.dt.uint8
FP8X4 = mybir.dt.float8_e4m3fn_x4
FP4X4 = mybir.dt.float4_e2m1fn_x4
ALU = mybir.AluOpType
ACT = mybir.ActivationFunctionType
AX = mybir.AxisListType

P = 128
PACK = 4
PASSES = 2
K_PASS = P * PACK
NQ = 128
N = 512
T = 2048
GROUPS = N // P

SPAN = 256.0
ROWS_ON_VECTOR = 48
ROWS_FIRST = 96
SCALED_ON_VECTOR = 352

FLOPS = 2 * NQ * N * PASSES * K_PASS


def tile_attend_nrm_mask_topk_kernel(tc, qT, k_words, k_scales, mk, offs, out):
    nc = tc.nc
    with ExitStack() as ctx:
        sb = ctx.enter_context(tc.tile_pool(name="sb", bufs=1))
        psum = ctx.enter_context(tc.psum_pool(name="psum", bufs=1))

        offsets = sb.tile([P, N // 16], U16, name="offsets")
        nc.sync.dma_start(offsets[:], offs)

        scale_pool = sb.tile([P, T], U8, name="scale_pool", align_bytes=64)
        nc.scalar.dma_start(scale_pool[0:32, :].bitcast(I32), k_scales.bitcast(I32).rearrange("o f t -> f o t"))
        nc.vector.memset(scale_pool[32:64, :].bitcast(I32), 0)
        nc.vector.memset(scale_pool[64:P, :].bitcast(I32), 0)

        word_pool = sb.tile([P, T], I32, name="word_pool", align_bytes=64)
        words = k_words[0].rearrange("p t b -> p (t b)").bitcast(I32)
        nc.sync.dma_start(word_pool[:], words)

        q_raw = [sb.tile([P, K_PASS], F32, name=f"q_raw{o}", align_bytes=64) for o in range(PASSES)]
        for o in range(PASSES):
            nc.sync.dma_start(q_raw[o][:], qT[0, o * K_PASS:(o + 1) * K_PASS, :].rearrange("(p j) w -> p (j w)", j=PACK))
        mask = sb.tile([P, N], F32, name="mask", align_bytes=64)
        nc.sync.dma_start(mask[:, :N // 2], mk[0, :, :N // 2])

        k_planes = sb.tile([P, PASSES * N], U8, name="k_planes", align_bytes=64)
        nc.vector.memset(k_planes[:].bitcast(I32), 0)

        span = sb.tile([P, 1], F32, name="span")
        nc.vector.memset(span[:], SPAN)
        unit = sb.tile([P, 1], F32, name="unit", tag="early_codes", align_bytes=64)
        nc.vector.reciprocal(unit[:], span[:])
        last_unit = sb.tile([P, 1], F32, name="last_unit")
        nc.scalar.activation(last_unit[:], unit[:], ACT.Copy)

        picked = sb.tile([P, N], U8, name="picked", align_bytes=64)
        nc.vector.tensor_copy(picked[:], scale_pool[:].indirect(offsets[:]))
        for quad in range(4):
            queue = nc.sync if quad % 2 == 0 else nc.scalar
            queue.dma_start(k_planes[32 * quad:32 * quad + 4, :].bitcast(I32), picked[8 * quad:8 * quad + 8, :].bitcast(I32))
        for first in range(N // 2, N, P):
            nc.sync.dma_start(mask[:, first:first + P], mk[0, :, first:first + P])

        q_bf = sb.tile([P, PASSES, K_PASS], BF16, name="q_bf", align_bytes=64)
        q_codes = sb.tile([P, PASSES, NQ], U32, name="q_codes", align_bytes=64)
        q_planes = sb.tile([P, PASSES, NQ], U8, name="q_planes", align_bytes=64)

        def cast_views(o, rows):
            dst = q_bf[:, o, :].rearrange("p (w j) -> p w j", j=PACK)[:, rows, :]
            src = q_raw[o][:].rearrange("p (j w) -> p w j", j=PACK)[:, rows, :]
            return [view.rearrange("p (c i) j -> p c j i", i=4) for view in (dst, src)]

        nc.scalar.activation(*cast_views(0, slice(0, ROWS_FIRST)), ACT.Copy, scale=unit[:])
        nc.scalar.activation(*cast_views(0, slice(ROWS_FIRST, NQ)), ACT.Copy, scale=last_unit[:])
        nc.scalar.activation(*cast_views(1, slice(ROWS_ON_VECTOR, NQ)), ACT.Copy, scale=1.0 / SPAN)

        half = N // 2
        pairs = sb.tile([P, N], U32, name="pairs", align_bytes=64)
        halves = pairs[:].bitcast(U16).rearrange("p (n h) -> p h n", h=PASSES)
        for h in range(2):
            nc.vector.tensor_copy(
                pairs[:, h * half:(h + 1) * half],
                word_pool[:].bitcast(U32).indirect(offsets[:, h * half // 16:(h + 1) * half // 16]),
            )

        k_codes = {}

        def part(room, o, groups):
            width = len(groups) * P
            nc.vector.tensor_copy(room, halves[:, o, groups[0] * P:groups[0] * P + width])
            for i, group in enumerate(groups):
                k_codes[group, o] = room[:, i * P:(i + 1) * P]

        def quantise(o):
            nc.vector.quantize_mx(out=q_codes[:, o, :].bitcast(FP8X4), scales=q_planes[:, o, :], in_=q_bf[:, o, :])

        banks = [psum.tile([P, P], F32, name=f"scores{group}") for group in range(GROUPS)]

        def score(group, o):
            nc.tensor.matmul_mx(
                out=banks[group][:],
                lhsT=q_codes[:, o, :].bitcast(FP8X4),
                lhsT_scale=q_planes[:, o, :],
                rhs=k_codes[group, o].bitcast(FP4X4),
                rhs_scale=k_planes[:, o * N + group * P:o * N + (group + 1) * P],
                start=(o == 0),
                stop=(o == PASSES - 1),
            )

        early_codes = sb.tile([P, half], U16, name="early_codes", align_bytes=64)
        part(early_codes[:], 0, (0, 1))
        quantise(0)
        nc.vector.tensor_scalar(*cast_views(1, slice(0, ROWS_ON_VECTOR)), 1.0 / SPAN, None, ALU.mult)
        mid_codes = sb.tile([P, half], U16, name="mid_codes", tag="q_raw0", align_bytes=64)
        part(mid_codes[:, :P], 1, (0,))
        part(mid_codes[:, P:], 1, (1,))
        quantise(1)
        late_codes = sb.tile([P, N], U16, name="late_codes", tag="q_raw1", align_bytes=64)
        for i, (group, o) in enumerate(((2, 0), (2, 1), (3, 0), (3, 1))):
            part(late_codes[:, i * P:(i + 1) * P], o, (group,))
        for group, o in ((0, 0), (1, 0), (0, 1), (1, 1), (2, 0), (2, 1), (3, 0), (3, 1)):
            score(group, o)

        sunk = sb.tile([P, N], F32, name="sunk", align_bytes=64)
        tops = sb.tile([P, GROUPS], F32, name="tops")
        for together in ((0,), (1,), (2, 3)):
            for group in together:
                nc.vector.tensor_reduce(tops[:, group:group + 1], banks[group][:], AX.X, ALU.max)
            for group in together:
                cols = slice(group * P, (group + 1) * P)
                nc.vector.scalar_tensor_tensor(sunk[:, cols], mask[:, cols], 1.0, banks[group][:], ALU.subtract, ALU.add)
        shift = sb.tile([P, 1], F32, name="shift")
        shifts = sb.tile([P, GROUPS], F32, name="shifts")
        nc.vector.tensor_scalar(shifts[:], tops[:], -SPAN, None, ALU.mult, ALU.min, accum_out=shift[:])
        e = sb.tile([P, N], F32, name="e", align_bytes=64)
        total = sb.tile([P, 1], F32, name="total")
        nc.scalar.activation(e[:], sunk[:], ACT.Exp, bias=shift[:], scale=SPAN, accum_out=total[:])
        inv = sb.tile([P, 1], F32, name="inv")
        nc.vector.reciprocal(inv[:], total[:])
        res = sb.tile([P, N], F32, name="res", align_bytes=64)
        nc.vector.tensor_scalar(res[:, :half], e[:, :half], inv[:], None, ALU.mult)
        nc.sync.dma_start(out[0, :, :half], res[:, :half])
        nc.vector.tensor_scalar(res[:, half:SCALED_ON_VECTOR], e[:, half:SCALED_ON_VECTOR], inv[:], None, ALU.mult)
        nc.scalar.activation(res[:, SCALED_ON_VECTOR:], e[:, SCALED_ON_VECTOR:], ACT.Copy, scale=inv[:])
        nc.scalar.dma_start(out[0, :, half:], res[:, half:])
